import numpy as np
import ml_dtypes


def mxq(x, axis, fmt="e4m3"):
    dtype, down = {"e4m3": (ml_dtypes.float8_e4m3fn, 7), "e5m2": (ml_dtypes.float8_e5m2, 14)}[fmt]
    v = np.moveaxis(np.asarray(x, np.float32).astype(ml_dtypes.bfloat16).astype(np.float64), axis, -1)
    blocks = v.reshape(v.shape[:-1] + (-1, 32))
    amax = np.abs(blocks).max(-1, keepdims=True)
    byte = np.maximum(np.where(amax > 0, np.frexp(amax)[1] - 1 + 127, 0) - down, 1)
    scale = np.exp2(byte - 127.0)
    codes = (blocks / scale).astype(np.float32).astype(dtype).astype(np.float64)
    return np.moveaxis((codes * scale).reshape(v.shape), -1, axis)


WIDE = False


def mx_kscale(k, group=512):
    if not WIDE:
        return np.ones(k)
    levels = np.array([10, -10, 5, -5, 0])
    if group != 512:
        return np.exp2(np.random.permutation(np.resize(levels, k // group))).repeat(group)
    if k % 512:
        return np.exp2(np.random.permutation(np.resize(levels, k // 32))).repeat(32)
    a = np.empty((k // 512, 16))
    for p in range(k // 512):
        a[p, :8] = np.random.permutation(np.resize(levels, 8))
        for g in range(8):
            far = levels[np.abs(levels - a[p, g]) >= 10]
            a[p, g + 8] = far[np.random.randint(len(far))]
    return np.exp2(a.ravel()).repeat(32)


def f64(x):
    return np.asarray(x).astype(np.float64)


def striped(idx):
    return np.tile(np.asarray(idx).reshape(-1, 16).T, (8, 1)).astype(np.uint16)


def unstriped(offs):
    return offs[:16].T.reshape(-1).astype(np.int64)


H, KV, D, NQ, N = 8, 8, 128, 512, 512


def setup_inputs():
    n = np.random.standard_normal
    s = mx_kscale(D, 0)[:, None]
    u = mx_kscale(N)
    t = np.random.uniform(0.5, 2.0, N) * u
    v = n((KV, N, 128))
    return {
        "qT": (n((H, D, NQ)) * s * (0.70 / np.sqrt(D))).astype(np.float32),
        "kT": (n((KV, D, N)) / s).astype(np.float32),
        "t": t.reshape(N, 1).astype(np.float32),
        "v": (v / t[:, None]).astype(np.float32),
        "kb": (0.5 * n((N, 1))).astype(np.float32),
    }


def reference(qT, kT, t, v, kb):
    a = mxq(f64(kT), 1, "e4m3").transpose(0, 2, 1) @ mxq(f64(qT), 1, "e4m3")
    a = a + f64(kb)
    p = np.maximum(a, 0.0)
    w = p * f64(t)
    y = mxq(w, 1, "e4m3").transpose(0, 2, 1) @ mxq(f64(v), 1, "e4m3")
    y = y / 16.0
    return y

@@ -1,0 +1,452 @@
+from contextlib import ExitStack
+
+import concourse.mybir as mybir
+
+H, D, NQ, N = 8, 128, 512, 512
+FLOPS = 2 * 2 * H * D * NQ * N
+F32 = mybir.dt.float32
+BF16 = mybir.dt.bfloat16
+U32 = mybir.dt.uint32
+U8 = mybir.dt.uint8
+FP8X4 = mybir.dt.float8_e4m3fn_x4
+ALU = mybir.AluOpType
+ACT = mybir.ActivationFunctionType
+P = 128
+
+STEPS = [
+    ('load_t',),
+    ('load_q', 0, 0),
+    ('load_kb',),
+    ('load_k', 0, 0),
+    ('load_k', 0, 1),
+    ('load_q', 0, 1),
+    ('load_v', 0),
+    ('load_k', 1, 0),
+    ('load_k', 1, 1),
+    ('load_q', 1, 0),
+    ('load_q', 1, 1),
+    ('load_v', 1),
+    ('load_v', 2),
+    ('load_v', 3),
+    ('abs',),
+    ('tkb',),
+    ('sign',),
+    ('cast_q', 'V', 0, 0, 0, 256),
+    ('quant_q', 0, 0, 256),
+    ('cast_k', 'V', 0, 0, 0, 256),
+    ('cast_k', 'A', 0, 1, 176, 256),
+    ('cast_k', 'V', 0, 1, 0, 176),
+    ('quant_k', 0, 0, 1),
+    ('quant_k', 0, 1, 2),
+    ('cast_q', 'V', 0, 1, 0, 256),
+    ('score', 0, 0, 0, 0, 0),
+    ('score', 0, 0, 1, 0, 128),
+    ('score', 1, 0, 0, 1, 0),
+    ('score', 1, 0, 1, 1, 128),
+    ('score', 2, 0, 0, 2, 0),
+    ('score', 2, 0, 1, 2, 128),
+    ('score', 3, 0, 0, 3, 0),
+    ('score', 3, 0, 1, 3, 128),
+    ('weigh', 0, 0, 0, 256, 0, 0),
+    ('quant_k', 0, 2, 4),
+    ('quant_q', 0, 256, 512),
+    ('weigh', 1, 0, 0, 256, 1, 0),
+    ('cast_v', 0),
+    ('weigh', 2, 0, 0, 256, 2, 0),
+    ('score', 0, 0, 2, 4, 0),
+    ('weigh', 3, 0, 0, 256, 3, 0),
+    ('score', 0, 0, 3, 4, 128),
+    ('score', 1, 0, 2, 1, 0),
+    ('score', 1, 0, 3, 1, 128),
+    ('score', 2, 0, 2, 2, 0),
+    ('cast_v', 1),
+    ('score', 2, 0, 3, 2, 128),
+    ('score', 3, 0, 2, 5, 0),
+    ('score', 3, 0, 3, 5, 128),
+    ('score', 0, 1, 0, 0, 0),
+    ('weigh', 0, 0, 256, 512, 4, 0),
+    ('score', 0, 1, 1, 0, 128),
+    ('score', 0, 1, 2, 0, 256),
+    ('score', 0, 1, 3, 0, 384),
+    ('cast_k', 'V', 1, 0, 0, 256),
+    ('weigh', 1, 0, 256, 512, 1, 0),
+    ('weigh', 2, 0, 256, 512, 2, 0),
+    ('score', 1, 1, 0, 1, 0),
+    ('weigh', 3, 0, 256, 512, 5, 0),
+    ('quant_v', 0),
+    ('score', 1, 1, 1, 1, 128),
+    ('score', 1, 1, 2, 1, 256),
+    ('score', 1, 1, 3, 1, 384),
+    ('score', 0, 2, 0, 4, 0),
+    ('score', 0, 2, 1, 4, 128),
+    ('weigh', 0, 1, 0, 512, 0, 0),
+    ('score', 0, 2, 2, 4, 256),
+    ('cast_k', 'V', 1, 1, 0, 256),
+    ('score', 0, 2, 3, 4, 384),
+    ('score', 2, 1, 0, 2, 0),
+    ('score', 2, 1, 1, 2, 128),
+    ('score', 2, 1, 2, 2, 256),
+    ('score', 2, 1, 3, 2, 384),
+    ('weigh', 1, 1, 0, 512, 1, 0),
+    ('score', 0, 3, 0, 0, 0),
+    ('score', 0, 3, 1, 0, 128),
+    ('score', 0, 3, 2, 0, 256),
+    ('cast_q', 'V', 1, 0, 0, 256),
+    ('weigh', 0, 2, 0, 512, 4, 0),
+    ('score', 0, 3, 3, 0, 384),
+    ('score', 1, 2, 0, 1, 0),
+    ('score', 1, 2, 1, 1, 128),
+    ('score', 1, 2, 2, 1, 256),
+    ('quant_k', 1, 0, 4),
+    ('weigh', 2, 1, 0, 512, 2, 0),
+    ('score', 1, 2, 3, 1, 384),
+    ('score', 3, 1, 0, 3, 0),
+    ('score', 3, 1, 1, 3, 128),
+    ('score', 3, 1, 2, 3, 256),
+    ('score', 3, 1, 3, 3, 384),
+    ('weigh', 0, 3, 0, 512, 0, 0),
+    ('cast_q', 'V', 1, 1, 0, 256),
+    ('score', 2, 2, 0, 2, 0),
+    ('score', 2, 2, 1, 2, 128),
+    ('score', 2, 2, 2, 2, 256),
+    ('weigh', 1, 2, 0, 512, 1, 0),
+    ('score', 2, 2, 3, 2, 384),
+    ('weave', 'V', 0, 0, 512),
+    ('weigh', 3, 1, 0, 512, 3, 0),
+    ('score', 1, 3, 0, 1, 0),
+    ('score', 1, 3, 1, 1, 128),
+    ('score', 1, 3, 2, 1, 256),
+    ('weigh', 2, 2, 0, 512, 2, 0),
+    ('score', 1, 3, 3, 1, 384),
+    ('score', 3, 2, 0, 5, 0),
+    ('score', 3, 2, 1, 5, 128),
+    ('score', 3, 2, 2, 5, 256),
+    ('score', 3, 2, 3, 5, 384),
+    ('quant_q', 1, 0, 512),
+    ('weigh', 1, 3, 0, 512, 1, 0),
+    ('quant_w', 0, 0, 512),
+    ('score', 4, 0, 0, 4, 0),
+    ('weigh', 3, 2, 0, 512, 5, 0),
+    ('score', 4, 0, 1, 4, 128),
+    ('score', 4, 0, 2, 4, 256),
+    ('cast_v', 2),
+    ('score', 4, 0, 3, 4, 384),
+    ('score', 2, 3, 0, 2, 0),
+    ('score', 2, 3, 1, 2, 128),
+    ('score', 2, 3, 2, 2, 256),
+    ('score', 2, 3, 3, 2, 384),
+    ('pv', 0, 0, 6, 0),
+    ('pv', 0, 1, 6, 128),
+    ('weigh', 4, 0, 0, 512, 4, 0),
+    ('cast_v', 3),
+    ('pv', 0, 2, 6, 256),
+    ('pv', 0, 3, 6, 384),
+    ('score', 4, 1, 0, 0, 0),
+    ('score', 4, 1, 1, 0, 128),
+    ('weigh', 2, 3, 0, 512, 2, 0),
+    ('weave', 'V', 1, 0, 512),
+    ('score', 4, 1, 2, 0, 256),
+    ('score', 4, 1, 3, 0, 384),
+    ('score', 3, 3, 0, 3, 0),
+    ('score', 3, 3, 1, 3, 128),
+    ('score', 3, 3, 2, 3, 256),
+    ('score', 3, 3, 3, 3, 384),
+    ('score', 5, 0, 0, 1, 0),
+    ('score', 5, 0, 1, 1, 128),
+    ('score', 5, 0, 2, 1, 256),
+    ('score', 5, 0, 3, 1, 384),
+    ('score', 4, 2, 0, 4, 0),
+    ('score', 4, 2, 1, 4, 128),
+    ('out', 'A', 0, 0, 4, 6, 0),
+    ('score', 4, 2, 2, 4, 256),
+    ('score', 4, 2, 3, 4, 384),
+    ('weigh', 4, 1, 0, 512, 0, 0),
+    ('quant_v', 1),
+    ('store', 0, 0, 4),
+    ('quant_w', 1, 0, 512),
+    ('weigh', 3, 3, 0, 512, 3, 0),
+    ('cast_v', 4),
+    ('weigh', 5, 0, 0, 512, 1, 0),
+    ('pv', 1, 0, 7, 0),
+    ('pv', 1, 1, 7, 128),
+    ('pv', 1, 2, 7, 256),
+    ('weave', 'V', 2, 0, 512),
+    ('pv', 1, 3, 7, 384),
+    ('weigh', 4, 2, 0, 512, 4, 0),
+    ('score', 6, 0, 0, 2, 0),
+    ('score', 6, 0, 1, 2, 128),
+    ('score', 6, 0, 2, 2, 256),
+    ('score', 6, 0, 3, 2, 384),
+    ('score', 5, 1, 0, 1, 0),
+    ('score', 5, 1, 1, 1, 128),
+    ('score', 5, 1, 2, 1, 256),
+    ('out', 'A', 1, 0, 4, 7, 0),
+    ('score', 5, 1, 3, 1, 384),
+    ('score', 4, 3, 0, 0, 0),
+    ('score', 4, 3, 1, 0, 128),
+    ('score', 4, 3, 2, 0, 256),
+    ('score', 4, 3, 3, 0, 384),
+    ('cast_v', 5),
+    ('weigh', 6, 0, 0, 512, 2, 0),
+    ('store', 1, 0, 4),
+    ('quant_w', 2, 0, 512),
+    ('weigh', 5, 1, 0, 512, 1, 0),
+    ('weave', 'V', 3, 0, 512),
+    ('weigh', 4, 3, 0, 512, 0, 0),
+    ('pv', 2, 0, 6, 0),
+    ('pv', 2, 1, 6, 128),
+    ('pv', 2, 2, 6, 256),
+    ('pv', 2, 3, 6, 384),
+    ('score', 6, 1, 0, 2, 0),
+    ('score', 6, 1, 1, 2, 128),
+    ('score', 6, 1, 2, 2, 256),
+    ('out', 'A', 2, 0, 4, 6, 0),
+    ('quant_v', 2),
+    ('score', 6, 1, 3, 2, 384),
+    ('score', 5, 2, 0, 1, 0),
+    ('score', 5, 2, 1, 1, 128),
+    ('score', 5, 2, 2, 1, 256),
+    ('score', 5, 2, 3, 1, 384),
+    ('score', 7, 0, 0, 5, 0),
+    ('score', 7, 0, 1, 5, 128),
+    ('score', 7, 0, 2, 5, 256),
+    ('score', 7, 0, 3, 5, 384),
+    ('quant_w', 3, 0, 512),
+    ('weigh', 6, 1, 0, 512, 2, 0),
+    ('store', 2, 0, 4),
+    ('cast_v', 6),
+    ('weigh', 5, 2, 0, 512, 1, 0),
+    ('pv', 3, 0, 7, 0),
+    ('pv', 3, 1, 7, 128),
+    ('pv', 3, 2, 7, 256),
+    ('weave', 'V', 4, 0, 512),
+    ('pv', 3, 3, 7, 384),
+    ('weigh', 7, 0, 0, 512, 5, 0),
+    ('score', 6, 2, 0, 2, 0),
+    ('score', 6, 2, 1, 2, 128),
+    ('score', 6, 2, 2, 2, 256),
+    ('score', 6, 2, 3, 2, 384),
+    ('score', 5, 3, 0, 1, 0),
+    ('score', 5, 3, 1, 1, 128),
+    ('score', 5, 3, 2, 1, 256),
+    ('out', 'A', 3, 0, 4, 7, 0),
+    ('score', 5, 3, 3, 1, 384),
+    ('score', 7, 1, 0, 3, 0),
+    ('score', 7, 1, 1, 3, 128),
+    ('score', 7, 1, 2, 3, 256),
+    ('score', 7, 1, 3, 3, 384),
+    ('cast_v', 7),
+    ('weigh', 6, 2, 0, 512, 2, 0),
+    ('store', 3, 0, 4),
+    ('quant_w', 4, 0, 512),
+    ('weigh', 5, 3, 0, 512, 1, 0),
+    ('score', 6, 3, 0, 2, 0),
+    ('score', 6, 3, 1, 2, 128),
+    ('score', 6, 3, 2, 2, 256),
+    ('weigh', 7, 1, 0, 512, 3, 0),
+    ('score', 6, 3, 3, 2, 384),
+    ('pv', 4, 0, 6, 0),
+    ('weave', 'V', 5, 0, 512),
+    ('pv', 4, 1, 6, 128),
+    ('pv', 4, 2, 6, 256),
+    ('weigh', 6, 3, 0, 512, 2, 0),
+    ('pv', 4, 3, 6, 384),
+    ('score', 7, 2, 0, 5, 0),
+    ('score', 7, 2, 1, 5, 128),
+    ('score', 7, 2, 2, 5, 256),
+    ('out', 'A', 4, 0, 4, 6, 0),
+    ('score', 7, 2, 3, 5, 384),
+    ('score', 7, 3, 0, 3, 0),
+    ('quant_v', 3),
+    ('score', 7, 3, 1, 3, 128),
+    ('weigh', 7, 2, 0, 512, 5, 0),
+    ('quant_w', 5, 0, 512),
+    ('store', 4, 0, 4),
+    ('weigh', 7, 3, 0, 256, 3, 0),
+    ('weave', 'V', 6, 0, 512),
+    ('score', 7, 3, 2, 5, 0),
+    ('score', 7, 3, 3, 5, 128),
+    ('pv', 5, 0, 7, 0),
+    ('pv', 5, 1, 7, 128),
+    ('pv', 5, 2, 7, 256),
+    ('weigh', 7, 3, 256, 512, 5, 0),
+    ('pv', 5, 3, 7, 384),
+    ('weave', 'V', 7, 0, 256),
+    ('out', 'A', 5, 0, 4, 7, 0),
+    ('quant_w', 6, 0, 512),
+    ('store', 5, 0, 4),
+    ('quant_w', 7, 0, 256),
+    ('pv', 6, 0, 6, 0),
+    ('weave', 'V', 7, 256, 512),
+    ('pv', 6, 1, 6, 128),
+    ('pv', 6, 2, 6, 256),
+    ('pv', 6, 3, 6, 384),
+    ('pv', 7, 0, 7, 0),
+    ('pv', 7, 1, 7, 128),
+    ('out', 'A', 6, 0, 4, 6, 0),
+    ('quant_w', 7, 256, 512),
+    ('out', 'A', 7, 0, 2, 7, 0),
+    ('store', 6, 0, 4),
+    ('pv', 7, 2, 6, 0),
+    ('pv', 7, 3, 6, 128),
+    ('store', 7, 0, 2),
+    ('out', 'A', 7, 2, 4, 6, 0),
+    ('store', 7, 2, 4),
+]
+
+
+def tile_rows_a_relu_kb_kernel(tc, qT, kT, t, v, kb, out):
+    nc = tc.nc
+    with ExitStack() as ctx:
+        sb = ctx.enter_context(tc.tile_pool(name="sb", bufs=1))
+        ps = ctx.enter_context(tc.psum_pool(name="ps", bufs=1))
+        ctx.enter_context(tc.manual_schedule())
+
+        def tiles(prefix, count, shape, dtype):
+            return [sb.tile(shape, dtype, name="%s%d" % (prefix, i), align_bytes=64) for i in range(count)]
+
+        t_sb = sb.tile([P, 4], F32, name="t_sb")
+        kb_sb = sb.tile([P, 4], F32, name="kb_sb")
+        t_abs = sb.tile([P, 4], F32, name="t_abs")
+        t_kb = sb.tile([P, 4], F32, name="t_kb")
+        t_pos = sb.tile([P, 4], F32, name="t_pos")
+        t_sign = sb.tile([P, 4], F32, name="t_sign")
+        q_raw = tiles("q_raw", 4, [P, 4, 256], F32)
+        k_raw = tiles("k_raw", 4, [P, 4, 256], F32)
+        v_raw = tiles("v_raw", 4, [P, 2, 4, 128], F32)
+        q_bf = tiles("q_bf", 2, [P, 512, 4], BF16)
+        k_bf = tiles("k_bf", 2, [P, 4, 128, 4], BF16)
+        v_bf = tiles("v_bf", 4, [P, 2, 128, 4], BF16)
+        q_codes = tiles("q_codes", 2, [P, 512], U32)
+        k_codes = tiles("k_codes", 2, [P, 512], U32)
+        v_codes = tiles("v_codes", 4, [P, 256], U32)
+        q_scales = tiles("q_scales", 2, [P, 512], U8)
+        k_scales = tiles("k_scales", 2, [P, 512], U8)
+        v_scales = tiles("v_scales", 4, [P, 256], U8)
+        w_rows = tiles("w_rows", H, [P, 4, 512], BF16)
+        w_bf = tiles("w_bf", H, [P, 512, 4], BF16)
+        w_codes = tiles("w_codes", H, [P, 512], U32)
+        w_scales = tiles("w_scales", H, [P, 512], U8)
+        y_sb = tiles("y_sb", H, [P, 4, 128], F32)
+        banks = [ps.tile([P, 512], F32, name="bank%d" % i) for i in range(8)]
+
+        def engine(e):
+            return nc.vector.tensor_copy if e == "V" else nc.scalar.copy
+
+        def quantize(codes, scales, src):
+            nc.vector.quantize_mx(out=codes.bitcast(FP8X4), scales=scales, in_=src)
+
+        for step in STEPS:
+            kind = step[0]
+            if kind == "load_t":
+                nc.scalar.dma_start(out=t_sb[:], in_=t.rearrange("(p j) o -> p (j o)", j=4))
+            elif kind == "load_kb":
+                nc.scalar.dma_start(out=kb_sb[:], in_=kb.rearrange("(p j) o -> p (j o)", j=4))
+            elif kind == "abs":
+                nc.scalar.activation(out=t_abs[:], in_=t_sb[:], func=ACT.Abs)
+            elif kind == "tkb":
+                nc.gpsimd.tensor_tensor(out=t_kb[:], in0=t_abs[:], in1=kb_sb[:], op=ALU.mult)
+            elif kind == "sign":
+                nc.gpsimd.tensor_scalar(out=t_pos[:], in0=t_sb[:], scalar1=0.0, scalar2=2.0, op0=ALU.is_ge, op1=ALU.mult)
+                nc.gpsimd.tensor_scalar(out=t_sign[:], in0=t_pos[:], scalar1=1.0, scalar2=-1.0, op0=ALU.mult, op1=ALU.add)
+            elif kind == "load_q" or kind == "load_k":
+                g, u = step[1], step[2]
+                src = qT if kind == "load_q" else kT
+                dst = q_raw if kind == "load_q" else k_raw
+                rows = src[4 * g : 4 * g + 4].rearrange("h (p j) n -> (h p) j n", j=4)
+                nc.sync.dma_start(out=dst[2 * g + u][:], in_=rows[:, :, 256 * u : 256 * u + 256])
+            elif kind == "load_v":
+                u = step[1]
+                nc.sync.dma_start(
+                    out=v_raw[u][:].rearrange("p h j e -> p h (j e)"),
+                    in_=v[2 * u : 2 * u + 2].rearrange("h (p j) e -> p h (j e)", j=4),
+                )
+            elif kind == "cast_q":
+                e, g, u, a, b = step[1:]
+                engine(e)(
+                    out=q_bf[g][:, 256 * u + a : 256 * u + b, :].rearrange("p (c i) j -> p c j i", i=4),
+                    in_=q_raw[2 * g + u][:, :, a:b].rearrange("p j (c i) -> p c j i", i=4),
+                )
+            elif kind == "cast_k":
+                e, g, u, a, b = step[1:]
+                engine(e)(
+                    out=k_bf[g][:, :, 64 * u + a // 4 : 64 * u + b // 4, :].rearrange("p r s j -> p s j r"),
+                    in_=k_raw[2 * g + u][:, :, a:b].rearrange("p j (s r) -> p s j r", r=4),
+                )
+            elif kind == "cast_v":
+                h = step[1]
+                nc.vector.tensor_tensor(
+                    out=v_bf[h // 2][:, h % 2, :, :].rearrange("p (c i) j -> p c j i", i=4),
+                    in0=v_raw[h // 2][:, h % 2, :, :].rearrange("p j (c i) -> p c j i", i=4),
+                    in1=t_sign[:].rearrange("p (a j b) -> p a j b", a=1, b=1).to_broadcast([P, 32, 4, 4]),
+                    op=ALU.mult,
+                )
+            elif kind == "quant_q":
+                g, a, b = step[1:]
+                quantize(q_codes[g][:, a:b], q_scales[g][:, a:b], q_bf[g][:, a:b, :].rearrange("p n j -> p (n j)"))
+            elif kind == "quant_k":
+                g, a, b = step[1:]
+                quantize(
+                    k_codes[g][:, 128 * a : 128 * b],
+                    k_scales[g][:, 128 * a : 128 * b],
+                    k_bf[g][:, a:b, :, :].rearrange("p r s j -> p (r s j)"),
+                )
+            elif kind == "quant_v":
+                u = step[1]
+                quantize(v_codes[u][:], v_scales[u][:], v_bf[u][:].rearrange("p h e j -> p (h e j)"))
+            elif kind == "score":
+                h, r, c, bank, col = step[1:]
+                g, rows = h // 4, slice(32 * (h % 4), 32 * (h % 4) + 32)
+                nc.tensor.matmul_mx(
+                    out=banks[bank][:, col : col + 128],
+                    lhsT=k_codes[g][rows, 128 * r : 128 * r + 128].bitcast(FP8X4),
+                    lhsT_scale=k_scales[g][rows, 128 * r : 128 * r + 128],
+                    rhs=q_codes[g][rows, 128 * c : 128 * c + 128].bitcast(FP8X4),
+                    rhs_scale=q_scales[g][rows, 128 * c : 128 * c + 128],
+                    start=True,
+                    stop=True,
+                )
+            elif kind == "weigh":
+                h, r, a, b, bank, col = step[1:]
+                nc.scalar.activation(
+                    out=w_rows[h][:, r, a:b],
+                    in_=banks[bank][:, col : col + b - a],
+                    func=ACT.Relu,
+                    bias=t_kb[:, r : r + 1],
+                    scale=t_abs[:, r : r + 1],
+                )
+            elif kind == "weave":
+                e, h, a, b = step[1:]
+                engine(e)(
+                    out=w_bf[h][:, a:b, :].rearrange("p (c i) j -> p c j i", i=4),
+                    in_=w_rows[h][:, :, a:b].rearrange("p j (c i) -> p c j i", i=4),
+                )
+            elif kind == "quant_w":
+                h, a, b = step[1:]
+                quantize(w_codes[h][:, a:b], w_scales[h][:, a:b], w_bf[h][:, a:b, :].rearrange("p n j -> p (n j)"))
+            elif kind == "pv":
+                h, c, bank, col = step[1:]
+                e0 = 128 * (h % 2)
+                nc.tensor.matmul_mx(
+                    out=banks[bank][:, col : col + 128],
+                    lhsT=w_codes[h][:, 128 * c : 128 * c + 128].bitcast(FP8X4),
+                    lhsT_scale=w_scales[h][:, 128 * c : 128 * c + 128],
+                    rhs=v_codes[h // 2][:, e0 : e0 + 128].bitcast(FP8X4),
+                    rhs_scale=v_scales[h // 2][:, e0 : e0 + 128],
+                    start=True,
+                    stop=True,
+                )
+            elif kind == "out":
+                e, h, a, b, bank, col = step[1:]
+                dst = y_sb[h][:, a:b, :].rearrange("p c e -> p (c e)")
+                src = banks[bank][:, col : col + 128 * (b - a)]
+                if e == "V":
+                    nc.vector.tensor_scalar(out=dst, in0=src, scalar1=0.0625, scalar2=None, op0=ALU.mult)
+                else:
+                    nc.scalar.activation(out=dst, in_=src, func=ACT.Copy, scale=0.0625)
+            elif kind == "store":
+                h, a, b = step[1:]
+                nc.sync.dma_start(
+                    out=out[h].rearrange("(c p) e -> p c e", p=P)[:, a:b, :],
+                    in_=y_sb[h][:, a:b, :],
+                )

@@ -15,282 +15,271 @@ P = 128
 
 STEPS = [
     ('load_t',),
-    ('load_q', 0, 0),
+    ('load_k', 0),
+    ('load_q', 0, 0, 512),
+    ('load_v', 0, 2),
+    ('load_k', 1),
+    ('load_q', 1, 0, 512),
+    ('load_v', 2, 8),
     ('load_kb',),
-    ('load_k', 0, 0),
-    ('load_k', 0, 1),
-    ('load_q', 0, 1),
-    ('load_v', 0),
-    ('load_k', 1, 0),
-    ('load_k', 1, 1),
-    ('load_q', 1, 0),
-    ('load_q', 1, 1),
-    ('load_v', 1),
-    ('load_v', 2),
-    ('load_v', 3),
     ('abs',),
     ('tkb',),
     ('sign',),
-    ('cast_q', 'V', 0, 0, 0, 256),
-    ('quant_q', 0, 0, 256),
-    ('cast_k', 'V', 0, 0, 0, 256),
-    ('cast_k', 'A', 0, 1, 176, 256),
-    ('cast_k', 'V', 0, 1, 0, 176),
-    ('quant_k', 0, 0, 1),
-    ('quant_k', 0, 1, 2),
-    ('cast_q', 'V', 0, 1, 0, 256),
-    ('score', 0, 0, 0, 0, 0),
-    ('score', 0, 0, 1, 0, 128),
-    ('score', 1, 0, 0, 1, 0),
-    ('score', 1, 0, 1, 1, 128),
-    ('score', 2, 0, 0, 2, 0),
-    ('score', 2, 0, 1, 2, 128),
+    ('cast_k', 'V', 0, 0, 4),
+    ('quant_k', 0, 0, 4),
+    ('cast_q', 'A', 0, 288, 512),
+    ('cast_q', 'V', 0, 0, 128),
+    ('cast_q', 'V', 0, 128, 288),
+    ('quant_q', 0, 0, 128),
+    ('quant_q', 0, 128, 256),
     ('score', 3, 0, 0, 3, 0),
-    ('score', 3, 0, 1, 3, 128),
-    ('weigh', 0, 0, 0, 256, 0, 0),
-    ('quant_k', 0, 2, 4),
     ('quant_q', 0, 256, 512),
-    ('weigh', 1, 0, 0, 256, 1, 0),
-    ('cast_v', 0),
-    ('weigh', 2, 0, 0, 256, 2, 0),
-    ('score', 0, 0, 2, 4, 0),
-    ('weigh', 3, 0, 0, 256, 3, 0),
-    ('score', 0, 0, 3, 4, 128),
-    ('score', 1, 0, 2, 1, 0),
-    ('score', 1, 0, 3, 1, 128),
-    ('score', 2, 0, 2, 2, 0),
-    ('cast_v', 1),
-    ('score', 2, 0, 3, 2, 128),
-    ('score', 3, 0, 2, 5, 0),
-    ('score', 3, 0, 3, 5, 128),
     ('score', 0, 1, 0, 0, 0),
-    ('weigh', 0, 0, 256, 512, 4, 0),
     ('score', 0, 1, 1, 0, 128),
-    ('score', 0, 1, 2, 0, 256),
-    ('score', 0, 1, 3, 0, 384),
-    ('cast_k', 'V', 1, 0, 0, 256),
-    ('weigh', 1, 0, 256, 512, 1, 0),
-    ('weigh', 2, 0, 256, 512, 2, 0),
-    ('score', 1, 1, 0, 1, 0),
-    ('weigh', 3, 0, 256, 512, 5, 0),
-    ('quant_v', 0),
-    ('score', 1, 1, 1, 1, 128),
-    ('score', 1, 1, 2, 1, 256),
-    ('score', 1, 1, 3, 1, 384),
-    ('score', 0, 2, 0, 4, 0),
-    ('score', 0, 2, 1, 4, 128),
-    ('weigh', 0, 1, 0, 512, 0, 0),
-    ('score', 0, 2, 2, 4, 256),
-    ('cast_k', 'V', 1, 1, 0, 256),
-    ('score', 0, 2, 3, 4, 384),
-    ('score', 2, 1, 0, 2, 0),
-    ('score', 2, 1, 1, 2, 128),
-    ('score', 2, 1, 2, 2, 256),
-    ('score', 2, 1, 3, 2, 384),
-    ('weigh', 1, 1, 0, 512, 1, 0),
+    ('cast_v', 0),
+    ('score', 3, 0, 1, 5, 0),
+    ('weigh', 3, 0, 0, 128, 3, 0),
+    ('score', 3, 0, 2, 5, 128),
+    ('weigh', 0, 1, 0, 256, 0, 0),
+    ('score', 3, 0, 3, 5, 256),
+    ('score', 0, 1, 2, 4, 0),
+    ('cast_v', 1),
+    ('score', 0, 1, 3, 4, 128),
+    ('score', 1, 0, 0, 1, 0),
+    ('weigh', 3, 0, 128, 512, 5, 0),
+    ('score', 1, 0, 1, 1, 128),
+    ('score', 1, 0, 2, 1, 256),
+    ('score', 1, 0, 3, 1, 384),
+    ('weigh', 0, 1, 256, 512, 4, 0),
+    ('score', 3, 1, 0, 3, 0),
+    ('quant_v', 0, 2),
+    ('score', 3, 1, 1, 3, 128),
+    ('score', 3, 1, 2, 3, 256),
+    ('weigh', 1, 0, 0, 512, 1, 0),
+    ('cast_k', 'V', 1, 0, 4),
+    ('score', 3, 1, 3, 3, 384),
+    ('score', 3, 3, 0, 5, 0),
+    ('score', 3, 3, 1, 5, 128),
+    ('score', 3, 3, 2, 5, 256),
+    ('weigh', 3, 1, 0, 512, 3, 0),
+    ('score', 3, 3, 3, 5, 384),
     ('score', 0, 3, 0, 0, 0),
     ('score', 0, 3, 1, 0, 128),
     ('score', 0, 3, 2, 0, 256),
-    ('cast_q', 'V', 1, 0, 0, 256),
-    ('weigh', 0, 2, 0, 512, 4, 0),
+    ('weigh', 3, 3, 0, 512, 5, 0),
     ('score', 0, 3, 3, 0, 384),
+    ('score', 3, 2, 0, 3, 0),
+    ('score', 3, 2, 1, 3, 128),
+    ('quant_k', 1, 0, 4),
+    ('score', 3, 2, 2, 3, 256),
+    ('weigh', 0, 3, 0, 512, 0, 0),
+    ('score', 3, 2, 3, 3, 384),
+    ('score', 1, 1, 0, 1, 0),
+    ('score', 1, 1, 1, 1, 128),
+    ('cast_q', 'V', 1, 0, 512),
+    ('score', 1, 1, 2, 1, 256),
+    ('weigh', 3, 2, 0, 512, 3, 0),
+    ('score', 1, 1, 3, 1, 384),
+    ('score', 2, 0, 0, 2, 0),
+    ('score', 2, 0, 1, 2, 128),
+    ('score', 2, 0, 2, 2, 256),
+    ('weigh', 1, 1, 0, 512, 1, 0),
+    ('score', 2, 0, 3, 2, 384),
+    ('score', 0, 0, 0, 4, 0),
+    ('score', 0, 0, 1, 4, 128),
+    ('weave', 'V', 3, 0, 512),
+    ('score', 0, 0, 2, 4, 256),
+    ('weigh', 2, 0, 0, 512, 2, 0),
+    ('score', 0, 0, 3, 4, 384),
     ('score', 1, 2, 0, 1, 0),
     ('score', 1, 2, 1, 1, 128),
     ('score', 1, 2, 2, 1, 256),
-    ('quant_k', 1, 0, 4),
-    ('weigh', 2, 1, 0, 512, 2, 0),
+    ('weigh', 0, 0, 0, 512, 4, 0),
     ('score', 1, 2, 3, 1, 384),
-    ('score', 3, 1, 0, 3, 0),
-    ('score', 3, 1, 1, 3, 128),
-    ('score', 3, 1, 2, 3, 256),
-    ('score', 3, 1, 3, 3, 384),
-    ('weigh', 0, 3, 0, 512, 0, 0),
-    ('cast_q', 'V', 1, 1, 0, 256),
-    ('score', 2, 2, 0, 2, 0),
-    ('score', 2, 2, 1, 2, 128),
-    ('score', 2, 2, 2, 2, 256),
+    ('score', 0, 2, 0, 0, 0),
+    ('score', 0, 2, 1, 0, 128),
+    ('quant_q', 1, 0, 512),
+    ('score', 0, 2, 2, 0, 256),
     ('weigh', 1, 2, 0, 512, 1, 0),
-    ('score', 2, 2, 3, 2, 384),
-    ('weave', 'V', 0, 0, 512),
-    ('weigh', 3, 1, 0, 512, 3, 0),
+    ('score', 0, 2, 3, 0, 384),
+    ('score', 2, 1, 0, 2, 0),
+    ('score', 2, 1, 1, 2, 128),
+    ('score', 2, 1, 2, 2, 256),
+    ('quant_w', 3, 0, 512),
+    ('weigh', 0, 2, 0, 512, 0, 0),
+    ('score', 2, 1, 3, 2, 384),
     ('score', 1, 3, 0, 1, 0),
     ('score', 1, 3, 1, 1, 128),
     ('score', 1, 3, 2, 1, 256),
-    ('weigh', 2, 2, 0, 512, 2, 0),
-    ('score', 1, 3, 3, 1, 384),
-    ('score', 3, 2, 0, 5, 0),
-    ('score', 3, 2, 1, 5, 128),
-    ('score', 3, 2, 2, 5, 256),
-    ('score', 3, 2, 3, 5, 384),
-    ('quant_q', 1, 0, 512),
-    ('weigh', 1, 3, 0, 512, 1, 0),
-    ('quant_w', 0, 0, 512),
-    ('score', 4, 0, 0, 4, 0),
-    ('weigh', 3, 2, 0, 512, 5, 0),
-    ('score', 4, 0, 1, 4, 128),
-    ('score', 4, 0, 2, 4, 256),
     ('cast_v', 2),
-    ('score', 4, 0, 3, 4, 384),
-    ('score', 2, 3, 0, 2, 0),
-    ('score', 2, 3, 1, 2, 128),
-    ('score', 2, 3, 2, 2, 256),
-    ('score', 2, 3, 3, 2, 384),
-    ('pv', 0, 0, 6, 0),
-    ('pv', 0, 1, 6, 128),
-    ('weigh', 4, 0, 0, 512, 4, 0),
+    ('weigh', 2, 1, 0, 512, 2, 0),
+    ('score', 1, 3, 3, 1, 384),
+    ('score', 4, 1, 0, 4, 0),
+    ('score', 4, 1, 1, 4, 128),
+    ('score', 4, 1, 2, 4, 256),
+    ('cast_v', 4),
+    ('weigh', 1, 3, 0, 512, 1, 0),
+    ('score', 4, 1, 3, 4, 384),
+    ('score', 2, 2, 0, 2, 0),
+    ('score', 2, 2, 1, 2, 128),
+    ('score', 2, 2, 2, 2, 256),
     ('cast_v', 3),
-    ('pv', 0, 2, 6, 256),
-    ('pv', 0, 3, 6, 384),
-    ('score', 4, 1, 0, 0, 0),
-    ('score', 4, 1, 1, 0, 128),
-    ('weigh', 2, 3, 0, 512, 2, 0),
-    ('weave', 'V', 1, 0, 512),
-    ('score', 4, 1, 2, 0, 256),
-    ('score', 4, 1, 3, 0, 384),
-    ('score', 3, 3, 0, 3, 0),
-    ('score', 3, 3, 1, 3, 128),
-    ('score', 3, 3, 2, 3, 256),
-    ('score', 3, 3, 3, 3, 384),
+    ('weigh', 4, 1, 0, 512, 4, 0),
+    ('score', 2, 2, 3, 2, 384),
     ('score', 5, 0, 0, 1, 0),
     ('score', 5, 0, 1, 1, 128),
     ('score', 5, 0, 2, 1, 256),
+    ('cast_v', 5),
+    ('weigh', 2, 2, 0, 512, 2, 0),
     ('score', 5, 0, 3, 1, 384),
-    ('score', 4, 2, 0, 4, 0),
-    ('score', 4, 2, 1, 4, 128),
-    ('out', 'A', 0, 0, 4, 6, 0),
-    ('score', 4, 2, 2, 4, 256),
-    ('score', 4, 2, 3, 4, 384),
-    ('weigh', 4, 1, 0, 512, 0, 0),
-    ('quant_v', 1),
-    ('store', 0, 0, 4),
-    ('quant_w', 1, 0, 512),
-    ('weigh', 3, 3, 0, 512, 3, 0),
-    ('cast_v', 4),
-    ('weigh', 5, 0, 0, 512, 1, 0),
-    ('pv', 1, 0, 7, 0),
-    ('pv', 1, 1, 7, 128),
-    ('pv', 1, 2, 7, 256),
-    ('weave', 'V', 2, 0, 512),
-    ('pv', 1, 3, 7, 384),
-    ('weigh', 4, 2, 0, 512, 4, 0),
-    ('score', 6, 0, 0, 2, 0),
-    ('score', 6, 0, 1, 2, 128),
-    ('score', 6, 0, 2, 2, 256),
-    ('score', 6, 0, 3, 2, 384),
-    ('score', 5, 1, 0, 1, 0),
-    ('score', 5, 1, 1, 1, 128),
-    ('score', 5, 1, 2, 1, 256),
-    ('out', 'A', 1, 0, 4, 7, 0),
-    ('score', 5, 1, 3, 1, 384),
     ('score', 4, 3, 0, 0, 0),
     ('score', 4, 3, 1, 0, 128),
     ('score', 4, 3, 2, 0, 256),
+    ('weave', 'V', 0, 0, 512),
+    ('weigh', 5, 0, 0, 512, 1, 0),
     ('score', 4, 3, 3, 0, 384),
-    ('cast_v', 5),
-    ('weigh', 6, 0, 0, 512, 2, 0),
-    ('store', 1, 0, 4),
-    ('quant_w', 2, 0, 512),
-    ('weigh', 5, 1, 0, 512, 1, 0),
-    ('weave', 'V', 3, 0, 512),
+    ('score', 2, 3, 0, 2, 0),
+    ('score', 2, 3, 1, 2, 128),
+    ('score', 2, 3, 2, 2, 256),
     ('weigh', 4, 3, 0, 512, 0, 0),
-    ('pv', 2, 0, 6, 0),
-    ('pv', 2, 1, 6, 128),
-    ('pv', 2, 2, 6, 256),
-    ('pv', 2, 3, 6, 384),
-    ('score', 6, 1, 0, 2, 0),
-    ('score', 6, 1, 1, 2, 128),
-    ('score', 6, 1, 2, 2, 256),
-    ('out', 'A', 2, 0, 4, 6, 0),
-    ('quant_v', 2),
-    ('score', 6, 1, 3, 2, 384),
+    ('score', 2, 3, 3, 2, 384),
+    ('score', 5, 1, 0, 1, 0),
+    ('score', 5, 1, 1, 1, 128),
+    ('score', 5, 1, 2, 1, 256),
+    ('weave', 'V', 1, 0, 512),
+    ('weigh', 2, 3, 0, 512, 2, 0),
+    ('score', 5, 1, 3, 1, 384),
+    ('score', 7, 1, 0, 5, 0),
+    ('score', 7, 1, 1, 5, 128),
+    ('score', 7, 1, 2, 5, 256),
+    ('weigh', 5, 1, 0, 512, 1, 0),
+    ('score', 7, 1, 3, 5, 384),
+    ('score', 6, 0, 0, 2, 0),
+    ('score', 6, 0, 1, 2, 128),
+    ('score', 6, 0, 2, 2, 256),
+    ('weigh', 7, 1, 0, 512, 5, 0),
+    ('quant_w', 0, 0, 512),
+    ('score', 6, 0, 3, 2, 384),
+    ('score', 4, 0, 0, 4, 0),
+    ('score', 4, 0, 1, 4, 128),
+    ('score', 4, 0, 2, 4, 256),
+    ('weigh', 6, 0, 0, 512, 2, 0),
+    ('cast_v', 6),
+    ('score', 4, 0, 3, 4, 384),
     ('score', 5, 2, 0, 1, 0),
     ('score', 5, 2, 1, 1, 128),
     ('score', 5, 2, 2, 1, 256),
+    ('weigh', 4, 0, 0, 512, 4, 0),
+    ('quant_v', 2, 6),
     ('score', 5, 2, 3, 1, 384),
-    ('score', 7, 0, 0, 5, 0),
-    ('score', 7, 0, 1, 5, 128),
-    ('score', 7, 0, 2, 5, 256),
-    ('score', 7, 0, 3, 5, 384),
-    ('quant_w', 3, 0, 512),
-    ('weigh', 6, 1, 0, 512, 2, 0),
-    ('store', 2, 0, 4),
-    ('cast_v', 6),
+    ('score', 4, 2, 0, 0, 0),
+    ('score', 4, 2, 1, 0, 128),
+    ('score', 4, 2, 2, 0, 256),
     ('weigh', 5, 2, 0, 512, 1, 0),
-    ('pv', 3, 0, 7, 0),
-    ('pv', 3, 1, 7, 128),
-    ('pv', 3, 2, 7, 256),
-    ('weave', 'V', 4, 0, 512),
-    ('pv', 3, 3, 7, 384),
-    ('weigh', 7, 0, 0, 512, 5, 0),
-    ('score', 6, 2, 0, 2, 0),
-    ('score', 6, 2, 1, 2, 128),
-    ('score', 6, 2, 2, 2, 256),
-    ('score', 6, 2, 3, 2, 384),
+    ('quant_w', 1, 0, 512),
+    ('score', 4, 2, 3, 0, 384),
+    ('score', 6, 1, 0, 2, 0),
+    ('score', 6, 1, 1, 2, 128),
+    ('score', 6, 1, 2, 2, 256),
+    ('weigh', 4, 2, 0, 512, 0, 0),
+    ('weave', 'V', 2, 0, 512),
+    ('score', 6, 1, 3, 2, 384),
     ('score', 5, 3, 0, 1, 0),
     ('score', 5, 3, 1, 1, 128),
     ('score', 5, 3, 2, 1, 256),
-    ('out', 'A', 3, 0, 4, 7, 0),
+    ('weigh', 6, 1, 0, 512, 2, 0),
     ('score', 5, 3, 3, 1, 384),
-    ('score', 7, 1, 0, 3, 0),
-    ('score', 7, 1, 1, 3, 128),
-    ('score', 7, 1, 2, 3, 256),
-    ('score', 7, 1, 3, 3, 384),
-    ('cast_v', 7),
-    ('weigh', 6, 2, 0, 512, 2, 0),
-    ('store', 3, 0, 4),
-    ('quant_w', 4, 0, 512),
+    ('pv', 3, 0, 6, 0),
+    ('pv', 3, 1, 6, 128),
+    ('pv', 3, 2, 6, 256),
     ('weigh', 5, 3, 0, 512, 1, 0),
+    ('pv', 3, 3, 6, 384),
+    ('weave', 'V', 4, 0, 512),
+    ('pv', 0, 0, 7, 0),
+    ('pv', 0, 1, 7, 128),
+    ('pv', 0, 2, 7, 256),
+    ('out', 'A', 3, 0, 4, 6, 0),
+    ('pv', 0, 3, 7, 384),
+    ('score', 6, 2, 0, 2, 0),
+    ('score', 6, 2, 1, 2, 128),
+    ('score', 6, 2, 2, 2, 256),
+    ('out', 'A', 0, 0, 4, 7, 0),
+    ('score', 6, 2, 3, 2, 384),
+    ('weave', 'V', 5, 0, 512),
+    ('store', 3, 0, 4),
+    ('score', 7, 2, 0, 3, 0),
+    ('score', 7, 2, 1, 3, 128),
+    ('score', 7, 2, 2, 3, 256),
+    ('weigh', 6, 2, 0, 512, 2, 0),
+    ('score', 7, 2, 3, 3, 384),
+    ('store', 0, 0, 4),
+    ('pv', 1, 0, 6, 0),
+    ('pv', 1, 1, 6, 128),
+    ('pv', 1, 2, 6, 256),
+    ('weigh', 7, 2, 0, 512, 3, 0),
+    ('pv', 1, 3, 6, 384),
+    ('quant_w', 4, 0, 512),
+    ('score', 7, 3, 0, 5, 0),
+    ('score', 7, 3, 1, 5, 128),
+    ('score', 7, 3, 2, 5, 256),
+    ('out', 'A', 1, 0, 4, 6, 0),
+    ('score', 7, 3, 3, 5, 384),
+    ('quant_w', 2, 0, 512),
     ('score', 6, 3, 0, 2, 0),
     ('score', 6, 3, 1, 2, 128),
     ('score', 6, 3, 2, 2, 256),
-    ('weigh', 7, 1, 0, 512, 3, 0),
+    ('weigh', 7, 3, 0, 512, 5, 0),
     ('score', 6, 3, 3, 2, 384),
-    ('pv', 4, 0, 6, 0),
-    ('weave', 'V', 5, 0, 512),
-    ('pv', 4, 1, 6, 128),
-    ('pv', 4, 2, 6, 256),
-    ('weigh', 6, 3, 0, 512, 2, 0),
-    ('pv', 4, 3, 6, 384),
-    ('score', 7, 2, 0, 5, 0),
-    ('score', 7, 2, 1, 5, 128),
-    ('score', 7, 2, 2, 5, 256),
-    ('out', 'A', 4, 0, 4, 6, 0),
-    ('score', 7, 2, 3, 5, 384),
-    ('score', 7, 3, 0, 3, 0),
-    ('quant_v', 3),
-    ('score', 7, 3, 1, 3, 128),
-    ('weigh', 7, 2, 0, 512, 5, 0),
     ('quant_w', 5, 0, 512),
-    ('store', 4, 0, 4),
-    ('weigh', 7, 3, 0, 256, 3, 0),
+    ('store', 1, 0, 4),
+    ('pv', 4, 0, 7, 0),
+    ('pv', 4, 1, 7, 128),
+    ('pv', 4, 2, 7, 256),
+    ('weigh', 6, 3, 0, 512, 2, 0),
+    ('pv', 4, 3, 7, 384),
+    ('cast_v', 7),
+    ('score', 7, 0, 0, 3, 0),
+    ('score', 7, 0, 1, 3, 128),
+    ('score', 7, 0, 2, 3, 256),
+    ('out', 'A', 4, 0, 4, 7, 0),
+    ('score', 7, 0, 3, 3, 384),
     ('weave', 'V', 6, 0, 512),
-    ('score', 7, 3, 2, 5, 0),
-    ('score', 7, 3, 3, 5, 128),
+    ('pv', 2, 0, 6, 0),
+    ('pv', 2, 1, 6, 128),
+    ('pv', 2, 2, 6, 256),
+    ('weigh', 7, 0, 0, 512, 3, 0),
+    ('pv', 2, 3, 6, 384),
+    ('store', 4, 0, 4),
     ('pv', 5, 0, 7, 0),
     ('pv', 5, 1, 7, 128),
     ('pv', 5, 2, 7, 256),
-    ('weigh', 7, 3, 256, 512, 5, 0),
+    ('out', 'A', 2, 0, 4, 6, 0),
     ('pv', 5, 3, 7, 384),
-    ('weave', 'V', 7, 0, 256),
+    ('quant_v', 6, 8),
     ('out', 'A', 5, 0, 4, 7, 0),
     ('quant_w', 6, 0, 512),
+    ('store', 2, 0, 4),
+    ('weave', 'A', 7, 256, 512),
+    ('weave', 'V', 7, 0, 256),
     ('store', 5, 0, 4),
-    ('quant_w', 7, 0, 256),
     ('pv', 6, 0, 6, 0),
-    ('weave', 'V', 7, 256, 512),
-    ('pv', 6, 1, 6, 128),
-    ('pv', 6, 2, 6, 256),
-    ('pv', 6, 3, 6, 384),
-    ('pv', 7, 0, 7, 0),
-    ('pv', 7, 1, 7, 128),
-    ('out', 'A', 6, 0, 4, 6, 0),
-    ('quant_w', 7, 256, 512),
-    ('out', 'A', 7, 0, 2, 7, 0),
-    ('store', 6, 0, 4),
-    ('pv', 7, 2, 6, 0),
-    ('pv', 7, 3, 6, 128),
+    ('pv', 6, 1, 7, 0),
+    ('pv', 6, 2, 7, 128),
+    ('pv', 6, 3, 7, 256),
+    ('out', 'V', 6, 0, 1, 6, 0),
+    ('quant_w', 7, 0, 256),
+    ('store', 6, 0, 1),
+    ('out', 'A', 6, 1, 4, 7, 0),
+    ('quant_w', 7, 256, 384),
+    ('pv', 7, 0, 6, 0),
+    ('pv', 7, 1, 6, 128),
+    ('quant_w', 7, 384, 512),
+    ('store', 6, 1, 4),
+    ('pv', 7, 2, 7, 0),
+    ('out', 'A', 7, 0, 2, 6, 0),
+    ('pv', 7, 3, 7, 128),
+    ('out', 'A', 7, 2, 4, 7, 0),
     ('store', 7, 0, 2),
-    ('out', 'A', 7, 2, 4, 6, 0),
     ('store', 7, 2, 4),
 ]
 
@@ -311,18 +300,18 @@ def tile_rows_a_relu_kb_kernel(tc, qT, kT, t, v, kb, out):
         t_kb = sb.tile([P, 4], F32, name="t_kb")
         t_pos = sb.tile([P, 4], F32, name="t_pos")
         t_sign = sb.tile([P, 4], F32, name="t_sign")
-        q_raw = tiles("q_raw", 4, [P, 4, 256], F32)
-        k_raw = tiles("k_raw", 4, [P, 4, 256], F32)
-        v_raw = tiles("v_raw", 4, [P, 2, 4, 128], F32)
+        q_raw = {}
+        k_raw = tiles("k_raw", 2, [P, 4, 512], F32)
+        v_raw = {}
         q_bf = tiles("q_bf", 2, [P, 512, 4], BF16)
         k_bf = tiles("k_bf", 2, [P, 4, 128, 4], BF16)
-        v_bf = tiles("v_bf", 4, [P, 2, 128, 4], BF16)
+        v_bf = sb.tile([P, H, 128, 4], BF16, name="v_bf", align_bytes=64)
         q_codes = tiles("q_codes", 2, [P, 512], U32)
         k_codes = tiles("k_codes", 2, [P, 512], U32)
-        v_codes = tiles("v_codes", 4, [P, 256], U32)
+        v_codes = sb.tile([P, H * 128], U32, name="v_codes", align_bytes=64)
         q_scales = tiles("q_scales", 2, [P, 512], U8)
         k_scales = tiles("k_scales", 2, [P, 512], U8)
-        v_scales = tiles("v_scales", 4, [P, 256], U8)
+        v_scales = sb.tile([P, H * 128], U8, name="v_scales", align_bytes=64)
         w_rows = tiles("w_rows", H, [P, 4, 512], BF16)
         w_bf = tiles("w_bf", H, [P, 512, 4], BF16)
         w_codes = tiles("w_codes", H, [P, 512], U32)
@@ -339,9 +328,9 @@ def tile_rows_a_relu_kb_kernel(tc, qT, kT, t, v, kb, out):
         for step in STEPS:
             kind = step[0]
             if kind == "load_t":
-                nc.scalar.dma_start(out=t_sb[:], in_=t.rearrange("(p j) o -> p (j o)", j=4))
+                nc.gpsimd.dma_start(out=t_sb[:], in_=t.rearrange("(p j) o -> p (j o)", j=4))
             elif kind == "load_kb":
-                nc.scalar.dma_start(out=kb_sb[:], in_=kb.rearrange("(p j) o -> p (j o)", j=4))
+                nc.gpsimd.dma_start(out=kb_sb[:], in_=kb.rearrange("(p j) o -> p (j o)", j=4))
             elif kind == "abs":
                 nc.scalar.activation(out=t_abs[:], in_=t_sb[:], func=ACT.Abs)
             elif kind == "tkb":
@@ -349,35 +338,46 @@ def tile_rows_a_relu_kb_kernel(tc, qT, kT, t, v, kb, out):
             elif kind == "sign":
                 nc.gpsimd.tensor_scalar(out=t_pos[:], in0=t_sb[:], scalar1=0.0, scalar2=2.0, op0=ALU.is_ge, op1=ALU.mult)
                 nc.gpsimd.tensor_scalar(out=t_sign[:], in0=t_pos[:], scalar1=1.0, scalar2=-1.0, op0=ALU.mult, op1=ALU.add)
-            elif kind == "load_q" or kind == "load_k":
-                g, u = step[1], step[2]
-                src = qT if kind == "load_q" else kT
-                dst = q_raw if kind == "load_q" else k_raw
-                rows = src[4 * g : 4 * g + 4].rearrange("h (p j) n -> (h p) j n", j=4)
-                nc.sync.dma_start(out=dst[2 * g + u][:], in_=rows[:, :, 256 * u : 256 * u + 256])
-            elif kind == "load_v":
-                u = step[1]
+            elif kind == "load_k":
+                g = step[1]
                 nc.sync.dma_start(
-                    out=v_raw[u][:].rearrange("p h j e -> p h (j e)"),
-                    in_=v[2 * u : 2 * u + 2].rearrange("h (p j) e -> p h (j e)", j=4),
+                    out=k_raw[g][:].rearrange("p j n -> p (j n)"),
+                    in_=kT[4 * g : 4 * g + 4].rearrange("h (p j) n -> (h p) (j n)", j=4),
+                )
+            elif kind == "load_q":
+                g, a, b = step[1:]
+                raw = sb.tile([P, 4, b - a], F32, name="q_raw%d_%d" % (g, a))
+                for n in range(a, b):
+                    q_raw[g, n] = (raw, a)
+                rows = qT[4 * g : 4 * g + 4].rearrange("h (p j) n -> (h p) j n", j=4)
+                nc.sync.dma_start(out=raw[:], in_=rows[:, :, a:b])
+            elif kind == "load_v":
+                a, b = step[1:]
+                raw = sb.tile([P, b - a, 4, 128], F32, name="v_raw%d" % a)
+                for h in range(a, b):
+                    v_raw[h] = raw[:, h - a, :, :]
+                nc.sync.dma_start(
+                    out=raw[:].rearrange("p h j e -> p h (j e)"),
+                    in_=v[a:b].rearrange("h (p j) e -> p h (j e)", j=4),
                 )
             elif kind == "cast_q":
-                e, g, u, a, b = step[1:]
+                e, g, a, b = step[1:]
+                raw, a0 = q_raw[g, a]
                 engine(e)(
-                    out=q_bf[g][:, 256 * u + a : 256 * u + b, :].rearrange("p (c i) j -> p c j i", i=4),
-                    in_=q_raw[2 * g + u][:, :, a:b].rearrange("p j (c i) -> p c j i", i=4),
+                    out=q_bf[g][:, a:b, :].rearrange("p (c i) j -> p c j i", i=4),
+                    in_=raw[:, :, a - a0 : b - a0].rearrange("p j (c i) -> p c j i", i=4),
                 )
             elif kind == "cast_k":
-                e, g, u, a, b = step[1:]
+                e, g, a, b = step[1:]
                 engine(e)(
-                    out=k_bf[g][:, :, 64 * u + a // 4 : 64 * u + b // 4, :].rearrange("p r s j -> p s j r"),
-                    in_=k_raw[2 * g + u][:, :, a:b].rearrange("p j (s r) -> p s j r", r=4),
+                    out=k_bf[g][:, a:b, :, :].rearrange("p r s j -> p s j r"),
+                    in_=k_raw[g][:].rearrange("p j (s r) -> p s j r", r=4)[:, :, :, a:b],
                 )
             elif kind == "cast_v":
                 h = step[1]
                 nc.vector.tensor_tensor(
-                    out=v_bf[h // 2][:, h % 2, :, :].rearrange("p (c i) j -> p c j i", i=4),
-                    in0=v_raw[h // 2][:, h % 2, :, :].rearrange("p j (c i) -> p c j i", i=4),
+                    out=v_bf[:, h, :, :].rearrange("p (c i) j -> p c j i", i=4),
+                    in0=v_raw[h].rearrange("p j (c i) -> p c j i", i=4),
                     in1=t_sign[:].rearrange("p (a j b) -> p a j b", a=1, b=1).to_broadcast([P, 32, 4, 4]),
                     op=ALU.mult,
                 )
@@ -392,8 +392,12 @@ def tile_rows_a_relu_kb_kernel(tc, qT, kT, t, v, kb, out):
                     k_bf[g][:, a:b, :, :].rearrange("p r s j -> p (r s j)"),
                 )
             elif kind == "quant_v":
-                u = step[1]
-                quantize(v_codes[u][:], v_scales[u][:], v_bf[u][:].rearrange("p h e j -> p (h e j)"))
+                a, b = step[1:]
+                quantize(
+                    v_codes[:, 128 * a : 128 * b],
+                    v_scales[:, 128 * a : 128 * b],
+                    v_bf[:, a:b, :, :].rearrange("p h e j -> p (h e j)"),
+                )
             elif kind == "score":
                 h, r, c, bank, col = step[1:]
                 g, rows = h // 4, slice(32 * (h % 4), 32 * (h % 4) + 32)
@@ -426,13 +430,13 @@ def tile_rows_a_relu_kb_kernel(tc, qT, kT, t, v, kb, out):
                 quantize(w_codes[h][:, a:b], w_scales[h][:, a:b], w_bf[h][:, a:b, :].rearrange("p n j -> p (n j)"))
             elif kind == "pv":
                 h, c, bank, col = step[1:]
-                e0 = 128 * (h % 2)
+                e0 = 128 * h
                 nc.tensor.matmul_mx(
                     out=banks[bank][:, col : col + 128],
                     lhsT=w_codes[h][:, 128 * c : 128 * c + 128].bitcast(FP8X4),
                     lhsT_scale=w_scales[h][:, 128 * c : 128 * c + 128],
-                    rhs=v_codes[h // 2][:, e0 : e0 + 128].bitcast(FP8X4),
-                    rhs_scale=v_scales[h // 2][:, e0 : e0 + 128],
+                    rhs=v_codes[:, e0 : e0 + 128].bitcast(FP8X4),
+                    rhs_scale=v_scales[:, e0 : e0 + 128],
                     start=True,
                     stop=True,
                 )

@@ -4,6 +4,7 @@ import concourse.mybir as mybir
 
 H, D, NQ, N = 8, 128, 512, 512
 FLOPS = 2 * 2 * H * D * NQ * N
+
 F32 = mybir.dt.float32
 BF16 = mybir.dt.bfloat16
 U32 = mybir.dt.uint32
@@ -11,281 +12,22 @@ U8 = mybir.dt.uint8
 FP8X4 = mybir.dt.float8_e4m3fn_x4
 ALU = mybir.AluOpType
 ACT = mybir.ActivationFunctionType
-P = 128
 
-STEPS = [
-    ('load_t',),
-    ('load_k', 0),
-    ('load_q', 0, 0, 512),
-    ('load_v', 0, 2),
-    ('load_k', 1),
-    ('load_q', 1, 0, 512),
-    ('load_v', 2, 8),
-    ('load_kb',),
-    ('abs',),
-    ('tkb',),
-    ('sign',),
-    ('cast_k', 'V', 0, 0, 4),
-    ('quant_k', 0, 0, 4),
-    ('cast_q', 'A', 0, 288, 512),
-    ('cast_q', 'V', 0, 0, 128),
-    ('cast_q', 'V', 0, 128, 288),
-    ('quant_q', 0, 0, 128),
-    ('quant_q', 0, 128, 256),
-    ('score', 3, 0, 0, 3, 0),
-    ('quant_q', 0, 256, 512),
-    ('score', 0, 1, 0, 0, 0),
-    ('score', 0, 1, 1, 0, 128),
-    ('cast_v', 0),
-    ('score', 3, 0, 1, 5, 0),
-    ('weigh', 3, 0, 0, 128, 3, 0),
-    ('score', 3, 0, 2, 5, 128),
-    ('weigh', 0, 1, 0, 256, 0, 0),
-    ('score', 3, 0, 3, 5, 256),
-    ('score', 0, 1, 2, 4, 0),
-    ('cast_v', 1),
-    ('score', 0, 1, 3, 4, 128),
-    ('score', 1, 0, 0, 1, 0),
-    ('weigh', 3, 0, 128, 512, 5, 0),
-    ('score', 1, 0, 1, 1, 128),
-    ('score', 1, 0, 2, 1, 256),
-    ('score', 1, 0, 3, 1, 384),
-    ('weigh', 0, 1, 256, 512, 4, 0),
-    ('score', 3, 1, 0, 3, 0),
-    ('quant_v', 0, 2),
-    ('score', 3, 1, 1, 3, 128),
-    ('score', 3, 1, 2, 3, 256),
-    ('weigh', 1, 0, 0, 512, 1, 0),
-    ('cast_k', 'V', 1, 0, 4),
-    ('score', 3, 1, 3, 3, 384),
-    ('score', 3, 3, 0, 5, 0),
-    ('score', 3, 3, 1, 5, 128),
-    ('score', 3, 3, 2, 5, 256),
-    ('weigh', 3, 1, 0, 512, 3, 0),
-    ('score', 3, 3, 3, 5, 384),
-    ('score', 0, 3, 0, 0, 0),
-    ('score', 0, 3, 1, 0, 128),
-    ('score', 0, 3, 2, 0, 256),
-    ('weigh', 3, 3, 0, 512, 5, 0),
-    ('score', 0, 3, 3, 0, 384),
-    ('score', 3, 2, 0, 3, 0),
-    ('score', 3, 2, 1, 3, 128),
-    ('quant_k', 1, 0, 4),
-    ('score', 3, 2, 2, 3, 256),
-    ('weigh', 0, 3, 0, 512, 0, 0),
-    ('score', 3, 2, 3, 3, 384),
-    ('score', 1, 1, 0, 1, 0),
-    ('score', 1, 1, 1, 1, 128),
-    ('cast_q', 'V', 1, 0, 512),
-    ('score', 1, 1, 2, 1, 256),
-    ('weigh', 3, 2, 0, 512, 3, 0),
-    ('score', 1, 1, 3, 1, 384),
-    ('score', 2, 0, 0, 2, 0),
-    ('score', 2, 0, 1, 2, 128),
-    ('score', 2, 0, 2, 2, 256),
-    ('weigh', 1, 1, 0, 512, 1, 0),
-    ('score', 2, 0, 3, 2, 384),
-    ('score', 0, 0, 0, 4, 0),
-    ('score', 0, 0, 1, 4, 128),
-    ('weave', 'V', 3, 0, 512),
-    ('score', 0, 0, 2, 4, 256),
-    ('weigh', 2, 0, 0, 512, 2, 0),
-    ('score', 0, 0, 3, 4, 384),
-    ('score', 1, 2, 0, 1, 0),
-    ('score', 1, 2, 1, 1, 128),
-    ('score', 1, 2, 2, 1, 256),
-    ('weigh', 0, 0, 0, 512, 4, 0),
-    ('score', 1, 2, 3, 1, 384),
-    ('score', 0, 2, 0, 0, 0),
-    ('score', 0, 2, 1, 0, 128),
-    ('quant_q', 1, 0, 512),
-    ('score', 0, 2, 2, 0, 256),
-    ('weigh', 1, 2, 0, 512, 1, 0),
-    ('score', 0, 2, 3, 0, 384),
-    ('score', 2, 1, 0, 2, 0),
-    ('score', 2, 1, 1, 2, 128),
-    ('score', 2, 1, 2, 2, 256),
-    ('quant_w', 3, 0, 512),
-    ('weigh', 0, 2, 0, 512, 0, 0),
-    ('score', 2, 1, 3, 2, 384),
-    ('score', 1, 3, 0, 1, 0),
-    ('score', 1, 3, 1, 1, 128),
-    ('score', 1, 3, 2, 1, 256),
-    ('cast_v', 2),
-    ('weigh', 2, 1, 0, 512, 2, 0),
-    ('score', 1, 3, 3, 1, 384),
-    ('score', 4, 1, 0, 4, 0),
-    ('score', 4, 1, 1, 4, 128),
-    ('score', 4, 1, 2, 4, 256),
-    ('cast_v', 4),
-    ('weigh', 1, 3, 0, 512, 1, 0),
-    ('score', 4, 1, 3, 4, 384),
-    ('score', 2, 2, 0, 2, 0),
-    ('score', 2, 2, 1, 2, 128),
-    ('score', 2, 2, 2, 2, 256),
-    ('cast_v', 3),
-    ('weigh', 4, 1, 0, 512, 4, 0),
-    ('score', 2, 2, 3, 2, 384),
-    ('score', 5, 0, 0, 1, 0),
-    ('score', 5, 0, 1, 1, 128),
-    ('score', 5, 0, 2, 1, 256),
-    ('cast_v', 5),
-    ('weigh', 2, 2, 0, 512, 2, 0),
-    ('score', 5, 0, 3, 1, 384),
-    ('score', 4, 3, 0, 0, 0),
-    ('score', 4, 3, 1, 0, 128),
-    ('score', 4, 3, 2, 0, 256),
-    ('weave', 'V', 0, 0, 512),
-    ('weigh', 5, 0, 0, 512, 1, 0),
-    ('score', 4, 3, 3, 0, 384),
-    ('score', 2, 3, 0, 2, 0),
-    ('score', 2, 3, 1, 2, 128),
-    ('score', 2, 3, 2, 2, 256),
-    ('weigh', 4, 3, 0, 512, 0, 0),
-    ('score', 2, 3, 3, 2, 384),
-    ('score', 5, 1, 0, 1, 0),
-    ('score', 5, 1, 1, 1, 128),
-    ('score', 5, 1, 2, 1, 256),
-    ('weave', 'V', 1, 0, 512),
-    ('weigh', 2, 3, 0, 512, 2, 0),
-    ('score', 5, 1, 3, 1, 384),
-    ('score', 7, 1, 0, 5, 0),
-    ('score', 7, 1, 1, 5, 128),
-    ('score', 7, 1, 2, 5, 256),
-    ('weigh', 5, 1, 0, 512, 1, 0),
-    ('score', 7, 1, 3, 5, 384),
-    ('score', 6, 0, 0, 2, 0),
-    ('score', 6, 0, 1, 2, 128),
-    ('score', 6, 0, 2, 2, 256),
-    ('weigh', 7, 1, 0, 512, 5, 0),
-    ('quant_w', 0, 0, 512),
-    ('score', 6, 0, 3, 2, 384),
-    ('score', 4, 0, 0, 4, 0),
-    ('score', 4, 0, 1, 4, 128),
-    ('score', 4, 0, 2, 4, 256),
-    ('weigh', 6, 0, 0, 512, 2, 0),
-    ('cast_v', 6),
-    ('score', 4, 0, 3, 4, 384),
-    ('score', 5, 2, 0, 1, 0),
-    ('score', 5, 2, 1, 1, 128),
-    ('score', 5, 2, 2, 1, 256),
-    ('weigh', 4, 0, 0, 512, 4, 0),
-    ('quant_v', 2, 6),
-    ('score', 5, 2, 3, 1, 384),
-    ('score', 4, 2, 0, 0, 0),
-    ('score', 4, 2, 1, 0, 128),
-    ('score', 4, 2, 2, 0, 256),
-    ('weigh', 5, 2, 0, 512, 1, 0),
-    ('quant_w', 1, 0, 512),
-    ('score', 4, 2, 3, 0, 384),
-    ('score', 6, 1, 0, 2, 0),
-    ('score', 6, 1, 1, 2, 128),
-    ('score', 6, 1, 2, 2, 256),
-    ('weigh', 4, 2, 0, 512, 0, 0),
-    ('weave', 'V', 2, 0, 512),
-    ('score', 6, 1, 3, 2, 384),
-    ('score', 5, 3, 0, 1, 0),
-    ('score', 5, 3, 1, 1, 128),
-    ('score', 5, 3, 2, 1, 256),
-    ('weigh', 6, 1, 0, 512, 2, 0),
-    ('score', 5, 3, 3, 1, 384),
-    ('pv', 3, 0, 6, 0),
-    ('pv', 3, 1, 6, 128),
-    ('pv', 3, 2, 6, 256),
-    ('weigh', 5, 3, 0, 512, 1, 0),
-    ('pv', 3, 3, 6, 384),
-    ('weave', 'V', 4, 0, 512),
-    ('pv', 0, 0, 7, 0),
-    ('pv', 0, 1, 7, 128),
-    ('pv', 0, 2, 7, 256),
-    ('out', 'A', 3, 0, 4, 6, 0),
-    ('pv', 0, 3, 7, 384),
-    ('score', 6, 2, 0, 2, 0),
-    ('score', 6, 2, 1, 2, 128),
-    ('score', 6, 2, 2, 2, 256),
-    ('out', 'A', 0, 0, 4, 7, 0),
-    ('score', 6, 2, 3, 2, 384),
-    ('weave', 'V', 5, 0, 512),
-    ('store', 3, 0, 4),
-    ('score', 7, 2, 0, 3, 0),
-    ('score', 7, 2, 1, 3, 128),
-    ('score', 7, 2, 2, 3, 256),
-    ('weigh', 6, 2, 0, 512, 2, 0),
-    ('score', 7, 2, 3, 3, 384),
-    ('store', 0, 0, 4),
-    ('pv', 1, 0, 6, 0),
-    ('pv', 1, 1, 6, 128),
-    ('pv', 1, 2, 6, 256),
-    ('weigh', 7, 2, 0, 512, 3, 0),
-    ('pv', 1, 3, 6, 384),
-    ('quant_w', 4, 0, 512),
-    ('score', 7, 3, 0, 5, 0),
-    ('score', 7, 3, 1, 5, 128),
-    ('score', 7, 3, 2, 5, 256),
-    ('out', 'A', 1, 0, 4, 6, 0),
-    ('score', 7, 3, 3, 5, 384),
-    ('quant_w', 2, 0, 512),
-    ('score', 6, 3, 0, 2, 0),
-    ('score', 6, 3, 1, 2, 128),
-    ('score', 6, 3, 2, 2, 256),
-    ('weigh', 7, 3, 0, 512, 5, 0),
-    ('score', 6, 3, 3, 2, 384),
-    ('quant_w', 5, 0, 512),
-    ('store', 1, 0, 4),
-    ('pv', 4, 0, 7, 0),
-    ('pv', 4, 1, 7, 128),
-    ('pv', 4, 2, 7, 256),
-    ('weigh', 6, 3, 0, 512, 2, 0),
-    ('pv', 4, 3, 7, 384),
-    ('cast_v', 7),
-    ('score', 7, 0, 0, 3, 0),
-    ('score', 7, 0, 1, 3, 128),
-    ('score', 7, 0, 2, 3, 256),
-    ('out', 'A', 4, 0, 4, 7, 0),
-    ('score', 7, 0, 3, 3, 384),
-    ('weave', 'V', 6, 0, 512),
-    ('pv', 2, 0, 6, 0),
-    ('pv', 2, 1, 6, 128),
-    ('pv', 2, 2, 6, 256),
-    ('weigh', 7, 0, 0, 512, 3, 0),
-    ('pv', 2, 3, 6, 384),
-    ('store', 4, 0, 4),
-    ('pv', 5, 0, 7, 0),
-    ('pv', 5, 1, 7, 128),
-    ('pv', 5, 2, 7, 256),
-    ('out', 'A', 2, 0, 4, 6, 0),
-    ('pv', 5, 3, 7, 384),
-    ('quant_v', 6, 8),
-    ('out', 'A', 5, 0, 4, 7, 0),
-    ('quant_w', 6, 0, 512),
-    ('store', 2, 0, 4),
-    ('weave', 'A', 7, 256, 512),
-    ('weave', 'V', 7, 0, 256),
-    ('store', 5, 0, 4),
-    ('pv', 6, 0, 6, 0),
-    ('pv', 6, 1, 7, 0),
-    ('pv', 6, 2, 7, 128),
-    ('pv', 6, 3, 7, 256),
-    ('out', 'V', 6, 0, 1, 6, 0),
-    ('quant_w', 7, 0, 256),
-    ('store', 6, 0, 1),
-    ('out', 'A', 6, 1, 4, 7, 0),
-    ('quant_w', 7, 256, 384),
-    ('pv', 7, 0, 6, 0),
-    ('pv', 7, 1, 6, 128),
-    ('quant_w', 7, 384, 512),
-    ('store', 6, 1, 4),
-    ('pv', 7, 2, 7, 0),
-    ('out', 'A', 7, 0, 2, 6, 0),
-    ('pv', 7, 3, 7, 128),
-    ('out', 'A', 7, 2, 4, 7, 0),
-    ('store', 7, 0, 2),
-    ('store', 7, 2, 4),
-]
+P = 128
+PACK = 4
+ROWS = 32
+COLS = 128
+GROUPS = H // PACK
+OUT_SCALE = 1.0 / 16.0
+
+SCORE_BANKS = ((0, 4), (1,), (2,), (3, 5))
+RESULT_BANKS = (6, 7)
 
 
 def tile_rows_a_relu_kb_kernel(tc, qT, kT, t, v, kb, out):
     nc = tc.nc
+    vector_copy, scalar_copy = nc.vector.tensor_copy, nc.scalar.copy
+
     with ExitStack() as ctx:
         sb = ctx.enter_context(tc.tile_pool(name="sb", bufs=1))
         ps = ctx.enter_context(tc.psum_pool(name="ps", bufs=1))
@@ -294,163 +36,254 @@ def tile_rows_a_relu_kb_kernel(tc, qT, kT, t, v, kb, out):
         def tiles(prefix, count, shape, dtype):
             return [sb.tile(shape, dtype, name="%s%d" % (prefix, i), align_bytes=64) for i in range(count)]
 
-        t_sb = sb.tile([P, 4], F32, name="t_sb")
-        kb_sb = sb.tile([P, 4], F32, name="kb_sb")
-        t_abs = sb.tile([P, 4], F32, name="t_abs")
-        t_kb = sb.tile([P, 4], F32, name="t_kb")
-        t_pos = sb.tile([P, 4], F32, name="t_pos")
-        t_sign = sb.tile([P, 4], F32, name="t_sign")
-        q_raw = {}
-        k_raw = tiles("k_raw", 2, [P, 4, 512], F32)
-        v_raw = {}
-        q_bf = tiles("q_bf", 2, [P, 512, 4], BF16)
-        k_bf = tiles("k_bf", 2, [P, 4, 128, 4], BF16)
-        v_bf = sb.tile([P, H, 128, 4], BF16, name="v_bf", align_bytes=64)
-        q_codes = tiles("q_codes", 2, [P, 512], U32)
-        k_codes = tiles("k_codes", 2, [P, 512], U32)
-        v_codes = sb.tile([P, H * 128], U32, name="v_codes", align_bytes=64)
-        q_scales = tiles("q_scales", 2, [P, 512], U8)
-        k_scales = tiles("k_scales", 2, [P, 512], U8)
-        v_scales = sb.tile([P, H * 128], U8, name="v_scales", align_bytes=64)
-        w_rows = tiles("w_rows", H, [P, 4, 512], BF16)
-        w_bf = tiles("w_bf", H, [P, 512, 4], BF16)
-        w_codes = tiles("w_codes", H, [P, 512], U32)
-        w_scales = tiles("w_scales", H, [P, 512], U8)
-        y_sb = tiles("y_sb", H, [P, 4, 128], F32)
+        t_sb = sb.tile([P, PACK], F32, name="t_sb")
+        kb_sb = sb.tile([P, PACK], F32, name="kb_sb")
+        t_abs = sb.tile([P, PACK], F32, name="t_abs")
+        t_abs_kb = sb.tile([P, PACK], F32, name="t_abs_kb")
+        t_step = sb.tile([P, PACK], F32, name="t_step")
+        t_sign = sb.tile([P, PACK], F32, name="t_sign")
+
+        q_bf = tiles("q_bf", GROUPS, [P, NQ, PACK], BF16)
+        k_bf = tiles("k_bf", GROUPS, [P, PACK, COLS, PACK], BF16)
+        v_bf = sb.tile([P, H, D, PACK], BF16, name="v_bf", align_bytes=64)
+        w_rows = tiles("w_rows", H, [P, PACK, NQ], BF16)
+        w_bf = tiles("w_bf", H, [P, NQ, PACK], BF16)
+        q_codes, q_scales = tiles("q_codes", GROUPS, [P, NQ], U32), tiles("q_scales", GROUPS, [P, NQ], U8)
+        k_codes, k_scales = tiles("k_codes", GROUPS, [P, N], U32), tiles("k_scales", GROUPS, [P, N], U8)
+        w_codes, w_scales = tiles("w_codes", H, [P, NQ], U32), tiles("w_scales", H, [P, NQ], U8)
+        v_codes = sb.tile([P, H * D], U32, name="v_codes", align_bytes=64)
+        v_scales = sb.tile([P, H * D], U8, name="v_scales", align_bytes=64)
+        y_sb = tiles("y_sb", H, [P, NQ // COLS, D], F32)
         banks = [ps.tile([P, 512], F32, name="bank%d" % i) for i in range(8)]
 
-        def engine(e):
-            return nc.vector.tensor_copy if e == "V" else nc.scalar.copy
+        loaded = []
+        v_raw = {}
+        uses = {}
 
-        def quantize(codes, scales, src):
-            nc.vector.quantize_mx(out=codes.bitcast(FP8X4), scales=scales, in_=src)
+        def take_bank(choice):
+            turn = uses.get(choice, 0)
+            uses[choice] = turn + 1
+            return banks[choice[turn % len(choice)]]
 
-        for step in STEPS:
-            kind = step[0]
-            if kind == "load_t":
-                nc.gpsimd.dma_start(out=t_sb[:], in_=t.rearrange("(p j) o -> p (j o)", j=4))
-            elif kind == "load_kb":
-                nc.gpsimd.dma_start(out=kb_sb[:], in_=kb.rearrange("(p j) o -> p (j o)", j=4))
-            elif kind == "abs":
-                nc.scalar.activation(out=t_abs[:], in_=t_sb[:], func=ACT.Abs)
-            elif kind == "tkb":
-                nc.gpsimd.tensor_tensor(out=t_kb[:], in0=t_abs[:], in1=kb_sb[:], op=ALU.mult)
-            elif kind == "sign":
-                nc.gpsimd.tensor_scalar(out=t_pos[:], in0=t_sb[:], scalar1=0.0, scalar2=2.0, op0=ALU.is_ge, op1=ALU.mult)
-                nc.gpsimd.tensor_scalar(out=t_sign[:], in0=t_pos[:], scalar1=1.0, scalar2=-1.0, op0=ALU.mult, op1=ALU.add)
-            elif kind == "load_k":
-                g = step[1]
-                nc.sync.dma_start(
-                    out=k_raw[g][:].rearrange("p j n -> p (j n)"),
-                    in_=kT[4 * g : 4 * g + 4].rearrange("h (p j) n -> (h p) (j n)", j=4),
-                )
-            elif kind == "load_q":
-                g, a, b = step[1:]
-                raw = sb.tile([P, 4, b - a], F32, name="q_raw%d_%d" % (g, a))
-                for n in range(a, b):
-                    q_raw[g, n] = (raw, a)
-                rows = qT[4 * g : 4 * g + 4].rearrange("h (p j) n -> (h p) j n", j=4)
-                nc.sync.dma_start(out=raw[:], in_=rows[:, :, a:b])
-            elif kind == "load_v":
-                a, b = step[1:]
-                raw = sb.tile([P, b - a, 4, 128], F32, name="v_raw%d" % a)
-                for h in range(a, b):
-                    v_raw[h] = raw[:, h - a, :, :]
-                nc.sync.dma_start(
-                    out=raw[:].rearrange("p h j e -> p h (j e)"),
-                    in_=v[a:b].rearrange("h (p j) e -> p h (j e)", j=4),
-                )
-            elif kind == "cast_q":
-                e, g, a, b = step[1:]
-                raw, a0 = q_raw[g, a]
-                engine(e)(
-                    out=q_bf[g][:, a:b, :].rearrange("p (c i) j -> p c j i", i=4),
-                    in_=raw[:, :, a - a0 : b - a0].rearrange("p j (c i) -> p c j i", i=4),
-                )
-            elif kind == "cast_k":
-                e, g, a, b = step[1:]
-                engine(e)(
-                    out=k_bf[g][:, a:b, :, :].rearrange("p r s j -> p s j r"),
-                    in_=k_raw[g][:].rearrange("p j (s r) -> p s j r", r=4)[:, :, :, a:b],
-                )
-            elif kind == "cast_v":
-                h = step[1]
-                nc.vector.tensor_tensor(
-                    out=v_bf[:, h, :, :].rearrange("p (c i) j -> p c j i", i=4),
-                    in0=v_raw[h].rearrange("p j (c i) -> p c j i", i=4),
-                    in1=t_sign[:].rearrange("p (a j b) -> p a j b", a=1, b=1).to_broadcast([P, 32, 4, 4]),
-                    op=ALU.mult,
-                )
-            elif kind == "quant_q":
-                g, a, b = step[1:]
-                quantize(q_codes[g][:, a:b], q_scales[g][:, a:b], q_bf[g][:, a:b, :].rearrange("p n j -> p (n j)"))
-            elif kind == "quant_k":
-                g, a, b = step[1:]
-                quantize(
-                    k_codes[g][:, 128 * a : 128 * b],
-                    k_scales[g][:, 128 * a : 128 * b],
-                    k_bf[g][:, a:b, :, :].rearrange("p r s j -> p (r s j)"),
-                )
-            elif kind == "quant_v":
-                a, b = step[1:]
-                quantize(
-                    v_codes[:, 128 * a : 128 * b],
-                    v_scales[:, 128 * a : 128 * b],
-                    v_bf[:, a:b, :, :].rearrange("p h e j -> p (h e j)"),
-                )
-            elif kind == "score":
-                h, r, c, bank, col = step[1:]
-                g, rows = h // 4, slice(32 * (h % 4), 32 * (h % 4) + 32)
+        def load_features(name, src, g, lo, hi):
+            raw = sb.tile([P, PACK, hi - lo], F32, name="%s_raw%d_%d" % (name, g, lo))
+            rows = src[PACK * g : PACK * (g + 1)].rearrange("h (p j) n -> (h p) j n", j=PACK)
+            nc.sync.dma_start(out=raw[:], in_=rows[:, :, lo:hi])
+            loaded.append((name, g, lo, hi, raw))
+
+        def raw_columns(name, g, lo, hi):
+            found = [x for x in loaded if x[0] == name and x[1] == g and x[2] <= lo and hi <= x[3]]
+            first, raw = found[0][2], found[0][4]
+            return raw[:, :, lo - first : hi - first]
+
+        def load_v(h0, h1):
+            raw = sb.tile([P, h1 - h0, PACK, D], F32, name="v_raw%d" % h0)
+            nc.sync.dma_start(
+                out=raw[:].rearrange("p h j e -> p h (j e)"),
+                in_=v[h0:h1].rearrange("h (p j) e -> p h (j e)", j=PACK),
+            )
+            for h in range(h0, h1):
+                v_raw[h] = raw[:, h - h0, :, :]
+
+        def round_q(copy, g, lo, hi):
+            copy(
+                out=q_bf[g][:, lo:hi, :].rearrange("p (c i) j -> p c j i", i=2),
+                in_=raw_columns("q", g, lo, hi).rearrange("p j (c i) -> p c j i", i=2),
+            )
+
+        def round_k(copy, g, lo, hi):
+            copy(
+                out=k_bf[g][:, :, lo // PACK : hi // PACK, :].rearrange("p r s j -> p s j r"),
+                in_=raw_columns("k", g, lo, hi).rearrange("p j (s r) -> p s j r", r=PACK),
+            )
+
+        def round_v(h):
+            nc.vector.tensor_tensor(
+                out=v_bf[:, h, :, :].rearrange("p (c i) j -> p c j i", i=2),
+                in0=v_raw[h].rearrange("p j (c i) -> p c j i", i=2),
+                in1=t_sign[:].rearrange("p (a j b) -> p a j b", a=1, b=1).to_broadcast([P, D // 2, PACK, 2]),
+                op=ALU.mult,
+            )
+
+        def interleave_w(copy, h, lo=0, hi=NQ):
+            copy(
+                out=w_bf[h][:, lo:hi, :].rearrange("p (c i) j -> p c j i", i=4),
+                in_=w_rows[h][:, :, lo:hi].rearrange("p j (c i) -> p c j i", i=4),
+            )
+
+        def quantize(codes, scales, values):
+            nc.vector.quantize_mx(out=codes.bitcast(FP8X4), scales=scales, in_=values)
+
+        def quantize_q(g, lo, hi):
+            quantize(q_codes[g][:, lo:hi], q_scales[g][:, lo:hi], q_bf[g][:, lo:hi, :].rearrange("p n j -> p (n j)"))
+
+        def quantize_k(g, r0, r1):
+            cols = slice(COLS * r0, COLS * r1)
+            quantize(k_codes[g][:, cols], k_scales[g][:, cols], k_bf[g][:, r0:r1, :, :].rearrange("p r s j -> p (r s j)"))
+
+        def quantize_v(h0, h1):
+            cols = slice(D * h0, D * h1)
+            quantize(v_codes[:, cols], v_scales[:, cols], v_bf[:, h0:h1, :, :].rearrange("p h e j -> p (h e j)"))
+
+        def quantize_w(h, lo=0, hi=NQ):
+            quantize(w_codes[h][:, lo:hi], w_scales[h][:, lo:hi], w_bf[h][:, lo:hi, :].rearrange("p n j -> p (n j)"))
+
+        def weigh(h, r, lo=0, hi=NQ):
+            g, rows = h // PACK, slice(ROWS * (h % PACK), ROWS * (h % PACK + 1))
+            tokens = slice(COLS * r, COLS * (r + 1))
+            bank = take_bank(SCORE_BANKS[h % PACK])
+            for q0 in range(lo, hi, COLS):
                 nc.tensor.matmul_mx(
-                    out=banks[bank][:, col : col + 128],
-                    lhsT=k_codes[g][rows, 128 * r : 128 * r + 128].bitcast(FP8X4),
-                    lhsT_scale=k_scales[g][rows, 128 * r : 128 * r + 128],
-                    rhs=q_codes[g][rows, 128 * c : 128 * c + 128].bitcast(FP8X4),
-                    rhs_scale=q_scales[g][rows, 128 * c : 128 * c + 128],
+                    out=bank[:, q0 - lo : q0 - lo + COLS],
+                    lhsT=k_codes[g][rows, tokens].bitcast(FP8X4),
+                    lhsT_scale=k_scales[g][rows, tokens],
+                    rhs=q_codes[g][rows, q0 : q0 + COLS].bitcast(FP8X4),
+                    rhs_scale=q_scales[g][rows, q0 : q0 + COLS],
                     start=True,
                     stop=True,
                 )
-            elif kind == "weigh":
-                h, r, a, b, bank, col = step[1:]
-                nc.scalar.activation(
-                    out=w_rows[h][:, r, a:b],
-                    in_=banks[bank][:, col : col + b - a],
-                    func=ACT.Relu,
-                    bias=t_kb[:, r : r + 1],
-                    scale=t_abs[:, r : r + 1],
-                )
-            elif kind == "weave":
-                e, h, a, b = step[1:]
-                engine(e)(
-                    out=w_bf[h][:, a:b, :].rearrange("p (c i) j -> p c j i", i=4),
-                    in_=w_rows[h][:, :, a:b].rearrange("p j (c i) -> p c j i", i=4),
-                )
-            elif kind == "quant_w":
-                h, a, b = step[1:]
-                quantize(w_codes[h][:, a:b], w_scales[h][:, a:b], w_bf[h][:, a:b, :].rearrange("p n j -> p (n j)"))
-            elif kind == "pv":
-                h, c, bank, col = step[1:]
-                e0 = 128 * h
+            nc.scalar.activation(
+                out=w_rows[h][:, r, lo:hi],
+                in_=bank[:, : hi - lo],
+                func=ACT.Relu,
+                bias=t_abs_kb[:, r : r + 1],
+                scale=t_abs[:, r : r + 1],
+            )
+
+        def second_product(h, c0, c1):
+            bank = take_bank(RESULT_BANKS)
+            for c in range(c0, c1):
                 nc.tensor.matmul_mx(
-                    out=banks[bank][:, col : col + 128],
-                    lhsT=w_codes[h][:, 128 * c : 128 * c + 128].bitcast(FP8X4),
-                    lhsT_scale=w_scales[h][:, 128 * c : 128 * c + 128],
-                    rhs=v_codes[:, e0 : e0 + 128].bitcast(FP8X4),
-                    rhs_scale=v_scales[:, e0 : e0 + 128],
+                    out=bank[:, D * (c - c0) : D * (c - c0 + 1)],
+                    lhsT=w_codes[h][:, COLS * c : COLS * (c + 1)].bitcast(FP8X4),
+                    lhsT_scale=w_scales[h][:, COLS * c : COLS * (c + 1)],
+                    rhs=v_codes[:, D * h : D * (h + 1)].bitcast(FP8X4),
+                    rhs_scale=v_scales[:, D * h : D * (h + 1)],
                     start=True,
                     stop=True,
                 )
-            elif kind == "out":
-                e, h, a, b, bank, col = step[1:]
-                dst = y_sb[h][:, a:b, :].rearrange("p c e -> p (c e)")
-                src = banks[bank][:, col : col + 128 * (b - a)]
-                if e == "V":
-                    nc.vector.tensor_scalar(out=dst, in0=src, scalar1=0.0625, scalar2=None, op0=ALU.mult)
-                else:
-                    nc.scalar.activation(out=dst, in_=src, func=ACT.Copy, scale=0.0625)
-            elif kind == "store":
-                h, a, b = step[1:]
-                nc.sync.dma_start(
-                    out=out[h].rearrange("(c p) e -> p c e", p=P)[:, a:b, :],
-                    in_=y_sb[h][:, a:b, :],
-                )
+            return bank[:, : D * (c1 - c0)], y_sb[h][:, c0:c1, :].rearrange("p c e -> p (c e)")
+
+        def result_on_scalar(h, c0=0, c1=PACK):
+            y, dst = second_product(h, c0, c1)
+            nc.scalar.activation(out=dst, in_=y, func=ACT.Copy, scale=OUT_SCALE)
+
+        def result_on_vector(h, c0=0, c1=PACK):
+            y, dst = second_product(h, c0, c1)
+            nc.vector.tensor_scalar(out=dst, in0=y, scalar1=OUT_SCALE, scalar2=None, op0=ALU.mult)
+
+        def store(h, c0=0, c1=PACK):
+            nc.sync.dma_start(out=out[h].rearrange("(c p) e -> p c e", p=P)[:, c0:c1, :], in_=y_sb[h][:, c0:c1, :])
+
+        nc.scalar.dma_start(out=t_sb[:], in_=t.rearrange("(p j) o -> p (j o)", j=PACK))
+        nc.scalar.dma_start(out=kb_sb[:], in_=kb.rearrange("(p j) o -> p (j o)", j=PACK))
+        load_features("k", kT, 0, 0, 256)
+        load_features("q", qT, 0, 0, 256)
+        load_features("k", kT, 0, 256, 512)
+        load_features("q", qT, 0, 256, 512)
+        load_v(0, 2)
+        load_features("k", kT, 1, 0, 512)
+        load_features("q", qT, 1, 0, 512)
+        load_v(2, 4)
+        load_v(4, 8)
+        nc.scalar.activation(out=t_abs[:], in_=t_sb[:], func=ACT.Abs)
+        nc.vector.tensor_scalar(out=t_step[:], in0=t_sb[:], scalar1=0.0, scalar2=2.0, op0=ALU.is_ge, op1=ALU.mult)
+        nc.vector.tensor_scalar(out=t_sign[:], in0=t_step[:], scalar1=-1.0, scalar2=None, op0=ALU.add)
+        nc.vector.tensor_tensor(out=t_abs_kb[:], in0=t_abs[:], in1=kb_sb[:], op=ALU.mult)
+        round_k(vector_copy, 0, 0, 256)
+        round_q(vector_copy, 0, 0, 256)
+        round_k(scalar_copy, 0, 384, 512)
+        round_k(vector_copy, 0, 256, 384)
+        quantize_q(0, 0, 256)
+        quantize_k(0, 0, 2)
+        round_q(scalar_copy, 0, 384, 512)
+        round_q(vector_copy, 0, 256, 384)
+        quantize_q(0, 256, 384)
+        quantize_q(0, 384, 512)
+        weigh(1, 0, 0, 256)
+        round_v(0)
+        round_v(1)
+        weigh(3, 0)
+        quantize_k(0, 2, 4)
+        weigh(2, 0)
+        quantize_v(0, 2)
+        weigh(1, 0, 256, 512)
+        round_k(vector_copy, 1, 0, 512)
+        weigh(0, 0)
+        weigh(3, 1)
+        weigh(1, 1)
+        quantize_k(1, 0, 4)
+        weigh(2, 1)
+        round_q(vector_copy, 1, 0, 512)
+        weigh(3, 2)
+        weigh(3, 3)
+        round_v(2)
+        weigh(1, 2)
+        quantize_q(1, 0, 512)
+        weigh(2, 2)
+        interleave_w(vector_copy, 3)
+        weigh(0, 1)
+        weigh(1, 3)
+        round_v(3)
+        weigh(0, 2)
+        round_v(4)
+        weigh(2, 3)
+        interleave_w(vector_copy, 1)
+        weigh(4, 0)
+        weigh(5, 0)
+        round_v(5)
+        weigh(4, 1)
+        quantize_w(1)
+        weigh(6, 0)
+        quantize_w(3)
+        weigh(0, 3)
+        round_v(6)
+        weigh(5, 1)
+        round_v(7)
+        weigh(4, 2)
+        interleave_w(vector_copy, 2)
+        weigh(7, 0)
+        weigh(4, 3)
+        interleave_w(vector_copy, 0)
+        weigh(5, 2)
+        weigh(7, 1)
+        quantize_v(2, 6)
+        weigh(6, 1)
+        quantize_w(2)
+        weigh(7, 2)
+        interleave_w(vector_copy, 4)
+        result_on_scalar(1)
+        weigh(5, 3)
+        store(1)
+        quantize_w(0)
+        weigh(6, 2)
+        interleave_w(vector_copy, 5)
+        result_on_scalar(2)
+        result_on_scalar(3)
+        store(2)
+        quantize_w(4)
+        weigh(6, 3)
+        store(3)
+        quantize_w(5)
+        result_on_scalar(0)
+        interleave_w(vector_copy, 6)
+        weigh(7, 3)
+        store(0)
+        result_on_scalar(4)
+        result_on_scalar(5)
+        quantize_v(6, 8)
+        store(4)
+        quantize_w(6)
+        interleave_w(scalar_copy, 7, 256, 512)
+        store(5)
+        interleave_w(vector_copy, 7, 0, 256)
+        result_on_vector(6, 0, 1)
+        quantize_w(7, 0, 256)
+        result_on_scalar(6, 1, 4)
+        quantize_w(7, 256, 384)
+        quantize_w(7, 384, 512)
+        store(6)
+        result_on_scalar(7, 0, 2)
+        result_on_scalar(7, 2, 4)
+        store(7, 0, 2)
+        store(7, 2, 4)

from contextlib import ExitStack

import concourse.mybir as mybir

H, D, NQ, N = 8, 128, 512, 512
FLOPS = 2 * 2 * H * D * NQ * N

F32 = mybir.dt.float32
BF16 = mybir.dt.bfloat16
U32 = mybir.dt.uint32
U8 = mybir.dt.uint8
FP8X4 = mybir.dt.float8_e4m3fn_x4
ALU = mybir.AluOpType
ACT = mybir.ActivationFunctionType

P = 128
PACK = 4
ROWS = 32
COLS = 128
GROUPS = H // PACK
OUT_SCALE = 1.0 / 16.0

SCORE_BANKS = ((0, 4), (1,), (2,), (3, 5))
RESULT_BANKS = (6, 7)


def tile_rows_a_relu_kb_kernel(tc, qT, kT, t, v, kb, out):
    nc = tc.nc
    vector_copy, scalar_copy = nc.vector.tensor_copy, nc.scalar.copy

    with ExitStack() as ctx:
        sb = ctx.enter_context(tc.tile_pool(name="sb", bufs=1))
        ps = ctx.enter_context(tc.psum_pool(name="ps", bufs=1))
        ctx.enter_context(tc.manual_schedule())

        def tiles(prefix, count, shape, dtype):
            return [sb.tile(shape, dtype, name="%s%d" % (prefix, i), align_bytes=64) for i in range(count)]

        t_sb = sb.tile([P, PACK], F32, name="t_sb")
        kb_sb = sb.tile([P, PACK], F32, name="kb_sb")
        t_abs = sb.tile([P, PACK], F32, name="t_abs")
        t_abs_kb = sb.tile([P, PACK], F32, name="t_abs_kb")
        t_step = sb.tile([P, PACK], F32, name="t_step")
        t_sign = sb.tile([P, PACK], F32, name="t_sign")

        q_bf = tiles("q_bf", GROUPS, [P, NQ, PACK], BF16)
        k_bf = tiles("k_bf", GROUPS, [P, PACK, COLS, PACK], BF16)
        v_bf = sb.tile([P, H, D, PACK], BF16, name="v_bf", align_bytes=64)
        w_rows = tiles("w_rows", H, [P, PACK, NQ], BF16)
        w_bf = tiles("w_bf", H, [P, NQ, PACK], BF16)
        q_codes, q_scales = tiles("q_codes", GROUPS, [P, NQ], U32), tiles("q_scales", GROUPS, [P, NQ], U8)
        k_codes, k_scales = tiles("k_codes", GROUPS, [P, N], U32), tiles("k_scales", GROUPS, [P, N], U8)
        w_codes, w_scales = tiles("w_codes", H, [P, NQ], U32), tiles("w_scales", H, [P, NQ], U8)
        v_codes = sb.tile([P, H * D], U32, name="v_codes", align_bytes=64)
        v_scales = sb.tile([P, H * D], U8, name="v_scales", align_bytes=64)
        y_sb = tiles("y_sb", H, [P, NQ // COLS, D], F32)
        banks = [ps.tile([P, 512], F32, name="bank%d" % i) for i in range(8)]

        loaded = []
        v_raw = {}
        uses = {}

        def take_bank(choice):
            turn = uses.get(choice, 0)
            uses[choice] = turn + 1
            return banks[choice[turn % len(choice)]]

        def load_features(name, src, g, lo, hi):
            raw = sb.tile([P, PACK, hi - lo], F32, name="%s_raw%d_%d" % (name, g, lo))
            rows = src[PACK * g : PACK * (g + 1)].rearrange("h (p j) n -> (h p) j n", j=PACK)
            nc.sync.dma_start(out=raw[:], in_=rows[:, :, lo:hi])
            loaded.append((name, g, lo, hi, raw))

        def raw_columns(name, g, lo, hi):
            found = [x for x in loaded if x[0] == name and x[1] == g and x[2] <= lo and hi <= x[3]]
            first, raw = found[0][2], found[0][4]
            return raw[:, :, lo - first : hi - first]

        def load_v(h0, h1):
            raw = sb.tile([P, h1 - h0, PACK, D], F32, name="v_raw%d" % h0)
            nc.sync.dma_start(
                out=raw[:].rearrange("p h j e -> p h (j e)"),
                in_=v[h0:h1].rearrange("h (p j) e -> p h (j e)", j=PACK),
            )
            for h in range(h0, h1):
                v_raw[h] = raw[:, h - h0, :, :]

        def round_q(copy, g, lo, hi):
            copy(
                out=q_bf[g][:, lo:hi, :].rearrange("p (c i) j -> p c j i", i=2),
                in_=raw_columns("q", g, lo, hi).rearrange("p j (c i) -> p c j i", i=2),
            )

        def round_k(copy, g, lo, hi):
            copy(
                out=k_bf[g][:, :, lo // PACK : hi // PACK, :].rearrange("p r s j -> p s j r"),
                in_=raw_columns("k", g, lo, hi).rearrange("p j (s r) -> p s j r", r=PACK),
            )

        def round_v(h):
            nc.vector.tensor_tensor(
                out=v_bf[:, h, :, :].rearrange("p (c i) j -> p c j i", i=2),
                in0=v_raw[h].rearrange("p j (c i) -> p c j i", i=2),
                in1=t_sign[:].rearrange("p (a j b) -> p a j b", a=1, b=1).to_broadcast([P, D // 2, PACK, 2]),
                op=ALU.mult,
            )

        def interleave_w(copy, h, lo=0, hi=NQ):
            copy(
                out=w_bf[h][:, lo:hi, :].rearrange("p (c i) j -> p c j i", i=4),
                in_=w_rows[h][:, :, lo:hi].rearrange("p j (c i) -> p c j i", i=4),
            )

        def quantize(codes, scales, values):
            nc.vector.quantize_mx(out=codes.bitcast(FP8X4), scales=scales, in_=values)

        def quantize_q(g, lo, hi):
            quantize(q_codes[g][:, lo:hi], q_scales[g][:, lo:hi], q_bf[g][:, lo:hi, :].rearrange("p n j -> p (n j)"))

        def quantize_k(g, r0, r1):
            cols = slice(COLS * r0, COLS * r1)
            quantize(k_codes[g][:, cols], k_scales[g][:, cols], k_bf[g][:, r0:r1, :, :].rearrange("p r s j -> p (r s j)"))

        def quantize_v(h0, h1):
            cols = slice(D * h0, D * h1)
            quantize(v_codes[:, cols], v_scales[:, cols], v_bf[:, h0:h1, :, :].rearrange("p h e j -> p (h e j)"))

        def quantize_w(h, lo=0, hi=NQ):
            quantize(w_codes[h][:, lo:hi], w_scales[h][:, lo:hi], w_bf[h][:, lo:hi, :].rearrange("p n j -> p (n j)"))

        def weigh(h, r, lo=0, hi=NQ):
            g, rows = h // PACK, slice(ROWS * (h % PACK), ROWS * (h % PACK + 1))
            tokens = slice(COLS * r, COLS * (r + 1))
            bank = take_bank(SCORE_BANKS[h % PACK])
            for q0 in range(lo, hi, COLS):
                nc.tensor.matmul_mx(
                    out=bank[:, q0 - lo : q0 - lo + COLS],
                    lhsT=k_codes[g][rows, tokens].bitcast(FP8X4),
                    lhsT_scale=k_scales[g][rows, tokens],
                    rhs=q_codes[g][rows, q0 : q0 + COLS].bitcast(FP8X4),
                    rhs_scale=q_scales[g][rows, q0 : q0 + COLS],
                    start=True,
                    stop=True,
                )
            nc.scalar.activation(
                out=w_rows[h][:, r, lo:hi],
                in_=bank[:, : hi - lo],
                func=ACT.Relu,
                bias=t_abs_kb[:, r : r + 1],
                scale=t_abs[:, r : r + 1],
            )

        def second_product(h, c0, c1):
            bank = take_bank(RESULT_BANKS)
            for c in range(c0, c1):
                nc.tensor.matmul_mx(
                    out=bank[:, D * (c - c0) : D * (c - c0 + 1)],
                    lhsT=w_codes[h][:, COLS * c : COLS * (c + 1)].bitcast(FP8X4),
                    lhsT_scale=w_scales[h][:, COLS * c : COLS * (c + 1)],
                    rhs=v_codes[:, D * h : D * (h + 1)].bitcast(FP8X4),
                    rhs_scale=v_scales[:, D * h : D * (h + 1)],
                    start=True,
                    stop=True,
                )
            return bank[:, : D * (c1 - c0)], y_sb[h][:, c0:c1, :].rearrange("p c e -> p (c e)")

        def result_on_scalar(h, c0=0, c1=PACK):
            y, dst = second_product(h, c0, c1)
            nc.scalar.activation(out=dst, in_=y, func=ACT.Copy, scale=OUT_SCALE)

        def result_on_vector(h, c0=0, c1=PACK):
            y, dst = second_product(h, c0, c1)
            nc.vector.tensor_scalar(out=dst, in0=y, scalar1=OUT_SCALE, scalar2=None, op0=ALU.mult)

        def store(h, c0=0, c1=PACK):
            nc.sync.dma_start(out=out[h].rearrange("(c p) e -> p c e", p=P)[:, c0:c1, :], in_=y_sb[h][:, c0:c1, :])

        nc.scalar.dma_start(out=t_sb[:], in_=t.rearrange("(p j) o -> p (j o)", j=PACK))
        nc.scalar.dma_start(out=kb_sb[:], in_=kb.rearrange("(p j) o -> p (j o)", j=PACK))
        load_features("k", kT, 0, 0, 256)
        load_features("q", qT, 0, 0, 256)
        load_features("k", kT, 0, 256, 512)
        load_features("q", qT, 0, 256, 512)
        load_v(0, 2)
        load_features("k", kT, 1, 0, 512)
        load_features("q", qT, 1, 0, 512)
        load_v(2, 4)
        load_v(4, 8)
        nc.scalar.activation(out=t_abs[:], in_=t_sb[:], func=ACT.Abs)
        nc.vector.tensor_scalar(out=t_step[:], in0=t_sb[:], scalar1=0.0, scalar2=2.0, op0=ALU.is_ge, op1=ALU.mult)
        nc.vector.tensor_scalar(out=t_sign[:], in0=t_step[:], scalar1=-1.0, scalar2=None, op0=ALU.add)
        nc.vector.tensor_tensor(out=t_abs_kb[:], in0=t_abs[:], in1=kb_sb[:], op=ALU.mult)
        round_k(vector_copy, 0, 0, 256)
        round_q(vector_copy, 0, 0, 256)
        round_k(scalar_copy, 0, 384, 512)
        round_k(vector_copy, 0, 256, 384)
        quantize_q(0, 0, 256)
        quantize_k(0, 0, 2)
        round_q(scalar_copy, 0, 384, 512)
        round_q(vector_copy, 0, 256, 384)
        quantize_q(0, 256, 384)
        quantize_q(0, 384, 512)
        weigh(1, 0, 0, 256)
        round_v(0)
        round_v(1)
        weigh(3, 0)
        quantize_k(0, 2, 4)
        weigh(2, 0)
        quantize_v(0, 2)
        weigh(1, 0, 256, 512)
        round_k(vector_copy, 1, 0, 512)
        weigh(0, 0)
        weigh(3, 1)
        weigh(1, 1)
        quantize_k(1, 0, 4)
        weigh(2, 1)
        round_q(vector_copy, 1, 0, 512)
        weigh(3, 2)
        weigh(3, 3)
        round_v(2)
        weigh(1, 2)
        quantize_q(1, 0, 512)
        weigh(2, 2)
        interleave_w(vector_copy, 3)
        weigh(0, 1)
        weigh(1, 3)
        round_v(3)
        weigh(0, 2)
        round_v(4)
        weigh(2, 3)
        interleave_w(vector_copy, 1)
        weigh(4, 0)
        weigh(5, 0)
        round_v(5)
        weigh(4, 1)
        quantize_w(1)
        weigh(6, 0)
        quantize_w(3)
        weigh(0, 3)
        round_v(6)
        weigh(5, 1)
        round_v(7)
        weigh(4, 2)
        interleave_w(vector_copy, 2)
        weigh(7, 0)
        weigh(4, 3)
        interleave_w(vector_copy, 0)
        weigh(5, 2)
        weigh(7, 1)
        quantize_v(2, 6)
        weigh(6, 1)
        quantize_w(2)
        weigh(7, 2)
        interleave_w(vector_copy, 4)
        result_on_scalar(1)
        weigh(5, 3)
        store(1)
        quantize_w(0)
        weigh(6, 2)
        interleave_w(vector_copy, 5)
        result_on_scalar(2)
        result_on_scalar(3)
        store(2)
        quantize_w(4)
        weigh(6, 3)
        store(3)
        quantize_w(5)
        result_on_scalar(0)
        interleave_w(vector_copy, 6)
        weigh(7, 3)
        store(0)
        result_on_scalar(4)
        result_on_scalar(5)
        quantize_v(6, 8)
        store(4)
        quantize_w(6)
        interleave_w(scalar_copy, 7, 256, 512)
        store(5)
        interleave_w(vector_copy, 7, 0, 256)
        result_on_vector(6, 0, 1)
        quantize_w(7, 0, 256)
        result_on_scalar(6, 1, 4)
        quantize_w(7, 256, 384)
        quantize_w(7, 384, 512)
        store(6)
        result_on_scalar(7, 0, 2)
        result_on_scalar(7, 2, 4)
        store(7, 0, 2)
        store(7, 2, 4)
